import numpy as np
import ml_dtypes


def mxq(x, axis, fmt="e4m3"):
    dtype, down = {"e4m3": (ml_dtypes.float8_e4m3fn, 7), "e5m2": (ml_dtypes.float8_e5m2, 14)}[fmt]
    v = np.moveaxis(np.asarray(x, np.float32).astype(ml_dtypes.bfloat16).astype(np.float64), axis, -1)
    blocks = v.reshape(v.shape[:-1] + (-1, 32))
    amax = np.abs(blocks).max(-1, keepdims=True)
    byte = np.maximum(np.where(amax > 0, np.frexp(amax)[1] - 1 + 127, 0) - down, 1)
    scale = np.exp2(byte - 127.0)
    codes = (blocks / scale).astype(np.float32).astype(dtype).astype(np.float64)
    return np.moveaxis((codes * scale).reshape(v.shape), -1, axis)


WIDE = False


def mx_kscale(k):
    if not WIDE:
        return np.ones(k)
    levels = np.array([10, -10, 5, -5, 0])
    if k % 512:
        return np.exp2(np.random.permutation(np.resize(levels, k // 32))).repeat(32)
    a = np.empty((k // 512, 16))
    for p in range(k // 512):
        a[p, :8] = np.random.permutation(np.resize(levels, 8))
        for g in range(8):
            far = levels[np.abs(levels - a[p, g]) >= 10]
            a[p, g + 8] = far[np.random.randint(len(far))]
    return np.exp2(a.ravel()).repeat(32)


def f64(x):
    return np.asarray(x).astype(np.float64)


def striped(idx):
    return np.tile(idx.reshape(-1, 16).T, (8, 1)).astype(np.uint16)


def unstriped(offs):
    return offs[:16].T.reshape(-1).astype(np.int64)


def pack_weight(w):
    k, n = w.shape
    w = f64(np.asarray(w, np.float32).astype(ml_dtypes.bfloat16)).reshape(k // 32, 32, n)
    amax = np.abs(w).max(1)
    byte = np.clip(np.where(amax > 0, np.frexp(amax)[1] - 1 + 127 - 7, 1), 1, 254)
    scaled = (w * np.exp2(127.0 - byte)[:, None, :]).reshape(k, n).astype(np.float32)
    words = np.ascontiguousarray(scaled.reshape(k // 512, 128, 4, n).transpose(0, 1, 3, 2)).astype(ml_dtypes.float8_e4m3fn).view(np.uint8)
    return words, np.ascontiguousarray(byte.astype(np.uint8).reshape(k // 512, 16, n))


def unpack_weight(words, scales):
    g, p, n, _ = words.shape
    vals = np.ascontiguousarray(words).view(ml_dtypes.float8_e4m3fn).astype(np.float64) * np.repeat(np.exp2(scales.astype(np.float64) - 127.0), 8, axis=1)[..., None]
    return vals.transpose(0, 1, 3, 2).reshape(g * 512, n)


def planes(y):
    n, m = y.shape
    v = y.astype(np.float32).astype(ml_dtypes.bfloat16).astype(np.float64).reshape(n // 32, 32, m)
    top = np.abs(v).max(1)
    byte = np.clip(np.where(top > 0, np.frexp(top)[1] - 1 + 127 - 7, 1), 1, 254)
    codes = (v * np.exp2(127.0 - byte)[:, None, :]).reshape(n, m).astype(np.float32).astype(ml_dtypes.float8_e4m3fn).view(np.uint8)
    words = codes.reshape(n // 512, 128, 4, m).transpose(0, 1, 3, 2)
    return np.ascontiguousarray(words), np.ascontiguousarray(byte.astype(np.uint8).reshape(n // 512, 16, m))


def relu(v):
    return np.maximum(v, 0.0)


K, T, S, V, H, N = 1024, 2048, 512, 256, 512, 512


def setup_inputs():
    n = np.random.standard_normal
    s = mx_kscale(K)[:, None]
    u = mx_kscale(H)
    near = np.random.permutation(S)
    packed_xT = pack_weight(n((K, T)) * s)
    return {
        "x_words": packed_xT[0],
        "x_scales": packed_xT[1],
        "w1": (n((K, H)) / np.sqrt(K) / s * u).astype(np.float32),
        "w2": (n((H, N)) / np.sqrt(H) / u[:, None]).astype(np.float32),
        "w3": (n((H, N)) / np.sqrt(H) / u[:, None]).astype(np.float32),
        "offs": striped(np.random.permutation(T)[:S]),
        "pos1": striped(near[:V]),
        "pos2": striped(near[V:]),
        "pos3": striped(np.random.permutation(S)[:V]),
    }


def reference(x_words, x_scales, w1, w2, w3, offs, pos1, pos2, pos3):
    xq = unpack_weight(x_words, x_scales)[:, unstriped(offs)]
    h = relu(mxq(f64(w1), 0, "e4m3").T @ xq)
    hq = mxq(h, 0, "e4m3")
    y = mxq(f64(w3), 0, "e4m3").T @ hq
    e = np.exp(mxq(f64(w2), 0, "e4m3").T @ hq)
    e0 = e[:, unstriped(pos1)]
    e1 = e[:, unstriped(pos2)]
    e2 = e[:, unstriped(pos3)]
    num = y[:, unstriped(pos1)] * e0 + y[:, unstriped(pos2)] * e1 + y[:, unstriped(pos3)] * e2
    den = e0 + e1 + e2
    out_0 = num / den
    return (out_0,) + planes(out_0)

@@ -1,0 +1,225 @@
+from contextlib import ExitStack
+
+import concourse.mybir as mybir
+
+K, T, S, V, H, N = 1024, 2048, 512, 256, 512, 512
+FLOPS = 2 * S * (K * H + 2 * H * N)
+
+F32 = mybir.dt.float32
+BF16 = mybir.dt.bfloat16
+I32 = mybir.dt.int32
+U32 = mybir.dt.uint32
+U16 = mybir.dt.uint16
+U8 = mybir.dt.uint8
+FP8X4 = mybir.dt.float8_e4m3fn_x4
+ACT = mybir.ActivationFunctionType
+ALU = mybir.AluOpType
+
+P = 128
+PACK = 4
+K_PASS = P * PACK
+PASSES = K // K_PASS
+QUADS = 4
+CHUNK = 128
+
+
+def tile_picked_zrandla_relu_po_kernel(
+    tc, x_words, x_scales, w1, w2, w3, offs, pos1, pos2, pos3, out_0, out_1, out_2
+):
+    nc = tc.nc
+    with ExitStack() as ctx:
+        keep = ctx.enter_context(tc.tile_pool(name="keep", bufs=1))
+        hpsum = ctx.enter_context(tc.psum_pool(name="hpsum", bufs=1))
+        mpsum = ctx.enter_context(tc.psum_pool(name="mpsum", bufs=4))
+
+        def load_list(src, name):
+            tile = keep.tile(list(src.shape), U16, name=name)
+            nc.sync.dma_start(tile[:], src)
+            return tile
+
+        def load_weight(rows, name):
+            raw = keep.tile([P, PACK, rows.shape[1]], F32, name=name, tag=name)
+            nc.sync.dma_start(out=raw[:], in_=rows.rearrange("(p j) c -> p j c", j=PACK))
+            return raw
+
+        def deal(engine, raw, name):
+            dealt = keep.tile([P, PACK, P, PACK], BF16, name=name, tag=name, align_bytes=64)
+            dst = dealt[:].rearrange("p t m j -> p m t j")
+            src = raw[:].rearrange("p j (m t) -> p m t j", t=PACK)
+            if engine == "scalar":
+                nc.scalar.activation(dst, src, ACT.Copy)
+            else:
+                nc.vector.tensor_copy(dst, src)
+            return dealt
+
+        def quantise(dealt, name):
+            codes = keep.tile([P, K_PASS], U32, name=name + "_codes", align_bytes=64)
+            scales = keep.tile([P, K_PASS], U8, name=name + "_scales", align_bytes=64)
+            nc.vector.quantize_mx(
+                out=codes[:].bitcast(FP8X4), scales=scales[:], in_=dealt[:].rearrange("p t m j -> p (t m j)")
+            )
+            return codes, scales
+
+        offs_sb = load_list(offs, "offs_sb")
+        xs_table = keep.tile([P, T], U8, name="xs_table")
+        nc.vector.memset(xs_table[:].bitcast(I32), 0)
+        w1_raw = [load_weight(w1[0:K_PASS, :], "w1_raw0")]
+        for q in range(QUADS):
+            nc.scalar.dma_start(
+                out=xs_table[32 * q : 32 * q + 4 * PASSES, :].bitcast(I32),
+                in_=x_scales.bitcast(I32)[:, 4 * q : 4 * q + 4, :],
+            )
+        w1_raw.append(load_weight(w1[K_PASS:K, :], "w1_raw1"))
+        xw_table = []
+        for g in range(PASSES):
+            table = keep.tile([P, T], U32, name="xw_table%d" % g)
+            nc.sync.dma_start(
+                out=table[:].bitcast(I32), in_=x_words[g].rearrange("p n t -> p (n t)").bitcast(I32)
+            )
+            xw_table.append(table)
+        w2_raw = load_weight(w2, "w2_raw")
+        pos_sb = [load_list(src, "pos%d_sb" % d) for d, src in enumerate((pos1, pos2, pos3))]
+        w3_raw = load_weight(w3, "w3_raw")
+
+        w1_q = []
+        xs = keep.tile([P, S], U8, name="xs", align_bytes=64)
+        nc.vector.tensor_copy(xs[:], xs_table[:].indirect(offs_sb[:]))
+        for g in range(PASSES):
+            w1_q.append(quantise(deal("scalar", w1_raw[g], "w1_dealt%d" % g), "w1_%d" % g))
+        xw = [keep.tile([P, S], U32, name="xw%d" % g, align_bytes=64) for g in range(PASSES)]
+        nc.vector.tensor_copy(xw[0][:], xw_table[0][:].indirect(offs_sb[:]))
+        for half in range(2):
+            nc.vector.tensor_copy(
+                xw[1][:, 256 * half : 256 * (half + 1)],
+                xw_table[1][:].indirect(offs_sb[:, 16 * half : 16 * (half + 1)]),
+            )
+
+        h_bf = keep.tile([P, S, PACK], BF16, name="h_bf", align_bytes=64)
+        h_codes = keep.tile([P, S], U32, name="h_codes", align_bytes=64)
+        h_scales = keep.tile([P, S], U8, name="h_scales", align_bytes=64)
+        for c in range(S // CHUNK):
+            cols = slice(c * CHUNK, (c + 1) * CHUNK)
+            bank = hpsum.tile([P, PACK, CHUNK], F32, name="h_bank%d" % c)
+            for t in range(PACK):
+                chans = slice(t * P, (t + 1) * P)
+                for g in range(PASSES):
+                    codes, scales = w1_q[g]
+                    nc.tensor.matmul_mx(
+                        out=bank[:, t, :],
+                        lhsT=codes[:, chans].bitcast(FP8X4),
+                        lhsT_scale=scales[:, chans],
+                        rhs=xw[g][:, cols].bitcast(FP8X4),
+                        rhs_scale=xs[4 * g : P, cols],
+                        start=(g == 0),
+                        stop=(g == PASSES - 1),
+                    )
+            nc.scalar.activation(h_bf[:, cols, :], bank[:].rearrange("p t n -> p n t"), ACT.Relu)
+            nc.vector.quantize_mx(
+                out=h_codes[:, cols].bitcast(FP8X4),
+                scales=h_scales[:, cols],
+                in_=h_bf[:, cols, :].rearrange("p n t -> p (n t)"),
+            )
+
+        def second_layer(w_q, t, name):
+            codes, scales = w_q
+            chans = slice(t * P, (t + 1) * P)
+            acc = mpsum.tile([P, S], F32, name="acc")
+            nc.tensor.matmul_mx(
+                out=acc[:],
+                lhsT=codes[:, chans].bitcast(FP8X4),
+                lhsT_scale=scales[:, chans],
+                rhs=h_codes[:].bitcast(FP8X4),
+                rhs_scale=h_scales[:],
+                start=True,
+                stop=True,
+            )
+            row = keep.tile([P, S], F32, name=name)
+            nc.scalar.copy(row[:], acc[:])
+            return row
+
+        def wide(name):
+            return keep.tile([P, PACK, V], F32, name=name)
+
+        def flat(tile, ts):
+            return tile[:, ts, :].rearrange("p t v -> p (t v)")
+
+        w2_q = quantise(deal("vector", w2_raw, "w2_dealt"), "w2")
+        score = [second_layer(w2_q, t, "score%d" % t) for t in range(PACK)]
+        w3_dealt = deal("scalar", w3_raw, "w3_dealt")
+
+        a, b = wide("a"), wide("b")
+        s0 = [keep.tile([P, V], F32, name="s0_%d" % t) for t in range(PACK - 1)]
+        th = keep.tile([P, PACK, V], F32, name="th", tag="w3_raw")
+        q1, q0, lg = wide("q1"), wide("q0"), wide("lg")
+        pairs = (slice(0, 2), slice(2, 4))
+        every = slice(0, PACK)
+
+        def pair_weights(ts):
+            nc.scalar.activation(flat(th, ts), flat(a, ts), ACT.Tanh, scale=0.5)
+            nc.scalar.activation(flat(q0, ts), flat(th, ts), ACT.Copy, scale=-0.5, bias=0.5)
+            nc.scalar.activation(flat(q1, ts), flat(th, ts), ACT.Copy, scale=0.5, bias=0.5)
+
+        def first(t):
+            nc.vector.tensor_copy(s0[t][:], score[t][:].indirect(pos_sb[0][:]))
+
+        def differences(t):
+            nc.vector.tensor_tensor(a[:, t, :], score[t][:].indirect(pos_sb[1][:]), s0[t][:], ALU.subtract)
+            nc.vector.tensor_tensor(b[:, t, :], score[t][:].indirect(pos_sb[2][:]), s0[t][:], ALU.subtract)
+
+        first(0)
+        first(1)
+        differences(0)
+        first(2)
+        differences(1)
+        pair_weights(pairs[0])
+        w3_q = quantise(w3_dealt, "w3")
+        feat = [second_layer(w3_q, t, "feat%d" % t) for t in range(2)]
+        s0.append(keep.tile([P, V], F32, name="s0_3", tag="w3_dealt", align_bytes=64))
+        first(3)
+        differences(2)
+        differences(3)
+        pair_weights(pairs[1])
+        feat = feat + [second_layer(w3_q, t, "feat%d" % t) for t in range(2, PACK)]
+
+        mag = wide("mag")
+        nc.scalar.activation(flat(mag, every), flat(th, every), ACT.Abs)
+        nc.scalar.activation(flat(lg, every), flat(mag, every), ACT.Ln, scale=0.5, bias=0.5)
+
+        r, z0, z1, y01, c2, th2, d2 = (wide(n) for n in ("r", "z0", "z1", "y01", "c2", "th2", "d2"))
+        nc.vector.scalar_tensor_tensor(flat(r, every), flat(a, every), 0.0, flat(b, every), ALU.max, ALU.subtract)
+        for t in range(PACK):
+            nc.vector.tensor_tensor(z0[:, t, :], feat[t][:].indirect(pos_sb[0][:]), q0[:, t, :], ALU.mult)
+            nc.vector.tensor_tensor(z1[:, t, :], feat[t][:].indirect(pos_sb[1][:]), q1[:, t, :], ALU.mult)
+        nc.vector.tensor_tensor(flat(c2, every), flat(lg, every), flat(r, every), ALU.subtract)
+        nc.vector.tensor_tensor(flat(y01, every), flat(z0, every), flat(z1, every), ALU.add)
+        nc.scalar.activation(flat(th2, every), flat(c2, every), ACT.Tanh, scale=0.5)
+        for t in range(PACK):
+            nc.vector.tensor_tensor(d2[:, t, :], feat[t][:].indirect(pos_sb[2][:]), y01[:, t, :], ALU.subtract)
+
+        o_codes = keep.tile([P, V], U32, name="o_codes", align_bytes=64)
+        o_scales = keep.tile([P, V], U8, name="o_scales", align_bytes=64)
+        out_rows = out_0.rearrange("(p t) v -> p t v", t=PACK)
+        words_out = out_1[0].rearrange("p n t -> p (n t)").bitcast(I32)
+        halves = [slice(0, V // 2), slice(V // 2, V)]
+        step = [keep.tile([P, PACK, V // 2], F32, name="step%d" % i) for i in range(2)]
+        res = [keep.tile([P, PACK, V // 2], F32, name="res%d" % i) for i in range(2)]
+        res_bf = [keep.tile([P, V // 2, PACK], BF16, name="res_bf%d" % i, align_bytes=64) for i in range(2)]
+        for i, vs in enumerate(halves):
+            nc.vector.scalar_tensor_tensor(step[i][:], th2[:, :, vs], 1.0, d2[:, :, vs], ALU.add, ALU.mult)
+        for i, vs in enumerate(halves):
+            nc.vector.scalar_tensor_tensor(res[i][:], step[i][:], 0.5, y01[:, :, vs], ALU.mult, ALU.add)
+            nc.sync.dma_start(out=out_rows[:, :, vs], in_=res[i][:])
+        nc.scalar.copy(res_bf[0][:], res[0][:].rearrange("p t v -> p v t"))
+        nc.vector.tensor_copy(res_bf[1][:], res[1][:].rearrange("p t v -> p v t"))
+        for i, vs in enumerate(halves):
+            nc.vector.quantize_mx(
+                out=o_codes[:, vs].bitcast(FP8X4),
+                scales=o_scales[:, vs],
+                in_=res_bf[i][:].rearrange("p v t -> p (v t)"),
+            )
+        nc.sync.dma_start(out=words_out, in_=o_codes[:].bitcast(I32))
+        for q in range(QUADS):
+            queue = nc.scalar if q % 2 else nc.sync
+            queue.dma_start(
+                out=out_2[0].bitcast(I32)[4 * q : 4 * q + 4, :], in_=o_scales[32 * q : 32 * q + 4, :].bitcast(I32)
+            )

@@ -42,22 +42,29 @@ def tile_picked_zrandla_relu_po_kernel(
             nc.sync.dma_start(out=raw[:], in_=rows.rearrange("(p j) c -> p j c", j=PACK))
             return raw
 
-        def deal(engine, raw, name):
-            dealt = keep.tile([P, PACK, P, PACK], BF16, name=name, tag=name, align_bytes=64)
-            dst = dealt[:].rearrange("p t m j -> p m t j")
-            src = raw[:].rearrange("p j (m t) -> p m t j", t=PACK)
-            if engine == "scalar":
+        def dealt_tile(name, tag):
+            return keep.tile([P, PACK, P, PACK], BF16, name=name, tag=tag, align_bytes=64)
+
+        def deal(on_scalar, dealt, raw, first):
+            count = raw.shape[2] // PACK
+            dst = dealt[:, :, first : first + count, :].rearrange("p t m j -> p m t j")
+            src = raw.rearrange("p j (m t) -> p m t j", t=PACK)
+            if on_scalar:
                 nc.scalar.activation(dst, src, ACT.Copy)
             else:
                 nc.vector.tensor_copy(dst, src)
-            return dealt
 
-        def quantise(dealt, name):
-            codes = keep.tile([P, K_PASS], U32, name=name + "_codes", align_bytes=64)
+        def quantise(dealt, name, pieces, tag):
+            codes = keep.tile([P, K_PASS], U32, name=name + "_codes", tag=tag, align_bytes=64)
             scales = keep.tile([P, K_PASS], U8, name=name + "_scales", align_bytes=64)
-            nc.vector.quantize_mx(
-                out=codes[:].bitcast(FP8X4), scales=scales[:], in_=dealt[:].rearrange("p t m j -> p (t m j)")
-            )
+            width = K_PASS // pieces
+            values = dealt[:].rearrange("p t m j -> p (t m j)")
+            for i in range(pieces):
+                nc.vector.quantize_mx(
+                    out=codes[:, i * width : (i + 1) * width].bitcast(FP8X4),
+                    scales=scales[:, i * width : (i + 1) * width],
+                    in_=values[:, PACK * i * width : PACK * (i + 1) * width],
+                )
             return codes, scales
 
         offs_sb = load_list(offs, "offs_sb")
@@ -65,7 +72,7 @@ def tile_picked_zrandla_relu_po_kernel(
         nc.vector.memset(xs_table[:].bitcast(I32), 0)
         w1_raw = [load_weight(w1[0:K_PASS, :], "w1_raw0")]
         for q in range(QUADS):
-            nc.scalar.dma_start(
+            nc.sync.dma_start(
                 out=xs_table[32 * q : 32 * q + 4 * PASSES, :].bitcast(I32),
                 in_=x_scales.bitcast(I32)[:, 4 * q : 4 * q + 4, :],
             )
@@ -77,7 +84,7 @@ def tile_picked_zrandla_relu_po_kernel(
                 out=table[:].bitcast(I32), in_=x_words[g].rearrange("p n t -> p (n t)").bitcast(I32)
             )
             xw_table.append(table)
-        w2_raw = load_weight(w2, "w2_raw")
+        w2_raw = [load_weight(w2[:, u * 256 : (u + 1) * 256], "w2_raw%d" % u) for u in range(2)]
         pos_sb = [load_list(src, "pos%d_sb" % d) for d, src in enumerate((pos1, pos2, pos3))]
         w3_raw = load_weight(w3, "w3_raw")
 
@@ -85,7 +92,10 @@ def tile_picked_zrandla_relu_po_kernel(
         xs = keep.tile([P, S], U8, name="xs", align_bytes=64)
         nc.vector.tensor_copy(xs[:], xs_table[:].indirect(offs_sb[:]))
         for g in range(PASSES):
-            w1_q.append(quantise(deal("scalar", w1_raw[g], "w1_dealt%d" % g), "w1_%d" % g))
+            w1_dealt = dealt_tile("w1_dealt%d" % g, "w1_dealt%d" % g)
+            deal(True, w1_dealt, w1_raw[g][:, :, 0:192], 0)
+            deal(False, w1_dealt, w1_raw[g][:, :, 192:512], 48)
+            w1_q.append(quantise(w1_dealt, "w1_%d" % g, 1, "w1_codes%d" % g))
         xw = [keep.tile([P, S], U32, name="xw%d" % g, align_bytes=64) for g in range(PASSES)]
         nc.vector.tensor_copy(xw[0][:], xw_table[0][:].indirect(offs_sb[:]))
         for half in range(2):
@@ -97,22 +107,45 @@ def tile_picked_zrandla_relu_po_kernel(
         h_bf = keep.tile([P, S, PACK], BF16, name="h_bf", align_bytes=64)
         h_codes = keep.tile([P, S], U32, name="h_codes", align_bytes=64)
         h_scales = keep.tile([P, S], U8, name="h_scales", align_bytes=64)
+        banks = [hpsum.tile([P, PACK, CHUNK], F32, name="h_bank%d" % c) for c in range(S // CHUNK)]
+
+        def first_layer_pass(c, t, g):
+            cols = slice(c * CHUNK, (c + 1) * CHUNK)
+            chans = slice(t * P, (t + 1) * P)
+            codes, scales = w1_q[g]
+            nc.tensor.matmul_mx(
+                out=banks[c][:, t, :],
+                lhsT=codes[:, chans].bitcast(FP8X4),
+                lhsT_scale=scales[:, chans],
+                rhs=xw[g][:, cols].bitcast(FP8X4),
+                rhs_scale=xs[4 * g : P, cols],
+                start=(g == 0),
+                stop=(g == PASSES - 1),
+            )
+
+        w2_dealt = dealt_tile("w2_dealt", "w2_dealt")
+        for c in range(S // CHUNK):
+            first_layer_pass(c, 0, 0)
+        warm = mpsum.tile([P, S], F32, name="acc")
+        for t in range(1, 3):
+            nc.tensor.matmul_mx(
+                out=warm[:],
+                lhsT=w1_q[0][0][:, t * P : (t + 1) * P].bitcast(FP8X4),
+                lhsT_scale=w1_q[0][1][:, t * P : (t + 1) * P],
+                rhs=xw[0][:].bitcast(FP8X4),
+                rhs_scale=xs[:],
+                start=True,
+                stop=True,
+            )
         for c in range(S // CHUNK):
             cols = slice(c * CHUNK, (c + 1) * CHUNK)
-            bank = hpsum.tile([P, PACK, CHUNK], F32, name="h_bank%d" % c)
-            for t in range(PACK):
-                chans = slice(t * P, (t + 1) * P)
+            bank = banks[c]
+            first_layer_pass(c, 0, 1)
+            for t in range(1, PACK):
                 for g in range(PASSES):
-                    codes, scales = w1_q[g]
-                    nc.tensor.matmul_mx(
-                        out=bank[:, t, :],
-                        lhsT=codes[:, chans].bitcast(FP8X4),
-                        lhsT_scale=scales[:, chans],
-                        rhs=xw[g][:, cols].bitcast(FP8X4),
-                        rhs_scale=xs[4 * g : P, cols],
-                        start=(g == 0),
-                        stop=(g == PASSES - 1),
-                    )
+                    first_layer_pass(c, t, g)
+            if c < 2:
+                deal(False, w2_dealt, w2_raw[c][:], 64 * c)
             nc.scalar.activation(h_bf[:, cols, :], bank[:].rearrange("p t n -> p n t"), ACT.Relu)
             nc.vector.quantize_mx(
                 out=h_codes[:, cols].bitcast(FP8X4),
@@ -120,22 +153,31 @@ def tile_picked_zrandla_relu_po_kernel(
                 in_=h_bf[:, cols, :].rearrange("p n t -> p (n t)"),
             )
 
-        def second_layer(w_q, t, name):
+        def product(acc, w_q, t, cols):
             codes, scales = w_q
             chans = slice(t * P, (t + 1) * P)
-            acc = mpsum.tile([P, S], F32, name="acc")
             nc.tensor.matmul_mx(
-                out=acc[:],
+                out=acc[:, cols],
                 lhsT=codes[:, chans].bitcast(FP8X4),
                 lhsT_scale=scales[:, chans],
-                rhs=h_codes[:].bitcast(FP8X4),
-                rhs_scale=h_scales[:],
+                rhs=h_codes[:, cols].bitcast(FP8X4),
+                rhs_scale=h_scales[:, cols],
                 start=True,
                 stop=True,
             )
+
+        def to_sbuf(acc, name, on_scalar):
             row = keep.tile([P, S], F32, name=name)
-            nc.scalar.copy(row[:], acc[:])
+            if on_scalar:
+                nc.scalar.copy(row[:], acc[:])
+            else:
+                nc.vector.tensor_copy(row[:], acc[:])
             return row
+
+        def second_layer(w_q, t, name):
+            acc = mpsum.tile([P, S], F32, name="acc")
+            product(acc, w_q, t, slice(0, S))
+            return to_sbuf(acc, name, True)
 
         def wide(name):
             return keep.tile([P, PACK, V], F32, name=name)
@@ -143,12 +185,17 @@ def tile_picked_zrandla_relu_po_kernel(
         def flat(tile, ts):
             return tile[:, ts, :].rearrange("p t v -> p (t v)")
 
-        w2_q = quantise(deal("vector", w2_raw, "w2_dealt"), "w2")
-        score = [second_layer(w2_q, t, "score%d" % t) for t in range(PACK)]
-        w3_dealt = deal("scalar", w3_raw, "w3_dealt")
+        w2_q = quantise(w2_dealt, "w2", PACK, "reused")
+        early = [mpsum.tile([P, S], F32, name="acc") for t in range(2)]
+        for cols in (slice(0, 256), slice(256, 384), slice(384, 512)):
+            for t in range(2):
+                product(early[t], w2_q, t, cols)
+        score = [to_sbuf(early[t], "score%d" % t, t > 0) for t in range(2)]
+        score = score + [second_layer(w2_q, t, "score%d" % t) for t in range(2, PACK)]
+        w3_dealt = dealt_tile("w3_dealt", "reused")
+        deal(True, w3_dealt, w3_raw[:], 0)
 
-        a, b = wide("a"), wide("b")
-        s0 = [keep.tile([P, V], F32, name="s0_%d" % t) for t in range(PACK - 1)]
+        s0, a = wide("s0"), wide("a")
         th = keep.tile([P, PACK, V], F32, name="th", tag="w3_raw")
         q1, q0, lg = wide("q1"), wide("q0"), wide("lg")
         pairs = (slice(0, 2), slice(2, 4))
@@ -160,38 +207,43 @@ def tile_picked_zrandla_relu_po_kernel(
             nc.scalar.activation(flat(q1, ts), flat(th, ts), ACT.Copy, scale=0.5, bias=0.5)
 
         def first(t):
-            nc.vector.tensor_copy(s0[t][:], score[t][:].indirect(pos_sb[0][:]))
+            nc.vector.tensor_copy(s0[:, t, :], score[t][:].indirect(pos_sb[0][:]))
 
-        def differences(t):
-            nc.vector.tensor_tensor(a[:, t, :], score[t][:].indirect(pos_sb[1][:]), s0[t][:], ALU.subtract)
-            nc.vector.tensor_tensor(b[:, t, :], score[t][:].indirect(pos_sb[2][:]), s0[t][:], ALU.subtract)
+        def difference(dst, t, d):
+            nc.vector.tensor_tensor(dst[:, t, :], score[t][:].indirect(pos_sb[d][:]), s0[:, t, :], ALU.subtract)
 
         first(0)
-        first(1)
-        differences(0)
-        first(2)
-        differences(1)
-        pair_weights(pairs[0])
-        w3_q = quantise(w3_dealt, "w3")
-        feat = [second_layer(w3_q, t, "feat%d" % t) for t in range(2)]
-        s0.append(keep.tile([P, V], F32, name="s0_3", tag="w3_dealt", align_bytes=64))
-        first(3)
-        differences(2)
-        differences(3)
-        pair_weights(pairs[1])
-        feat = feat + [second_layer(w3_q, t, "feat%d" % t) for t in range(2, PACK)]
+        for t in range(PACK):
+            if t + 1 < PACK:
+                first(t + 1)
+            difference(a, t, 1)
+        w3_q = quantise(w3_dealt, "w3", 1, "w3_codes")
+        b = keep.tile([P, PACK, V], F32, name="b", tag="reused", align_bytes=64)
+        for t in range(PACK):
+            difference(b, t, 2)
+        feat = []
+        for ts in pairs:
+            pair_weights(ts)
+            feat = feat + [second_layer(w3_q, t, "feat%d" % t) for t in range(ts.start, ts.stop)]
 
         mag = wide("mag")
         nc.scalar.activation(flat(mag, every), flat(th, every), ACT.Abs)
         nc.scalar.activation(flat(lg, every), flat(mag, every), ACT.Ln, scale=0.5, bias=0.5)
 
-        r, z0, z1, y01, c2, th2, d2 = (wide(n) for n in ("r", "z0", "z1", "y01", "c2", "th2", "d2"))
-        nc.vector.scalar_tensor_tensor(flat(r, every), flat(a, every), 0.0, flat(b, every), ALU.max, ALU.subtract)
-        for t in range(PACK):
+        z0, z1, y01, c2, th2 = (wide(n) for n in ("z0", "z1", "y01", "c2", "th2"))
+        r = keep.tile([P, PACK, V], F32, name="r", tag="r")
+
+        def weighted(t):
             nc.vector.tensor_tensor(z0[:, t, :], feat[t][:].indirect(pos_sb[0][:]), q0[:, t, :], ALU.mult)
             nc.vector.tensor_tensor(z1[:, t, :], feat[t][:].indirect(pos_sb[1][:]), q1[:, t, :], ALU.mult)
+
+        weighted(0)
+        nc.vector.scalar_tensor_tensor(flat(r, every), flat(a, every), 0.0, flat(b, every), ALU.max, ALU.subtract)
+        for t in range(1, PACK):
+            weighted(t)
         nc.vector.tensor_tensor(flat(c2, every), flat(lg, every), flat(r, every), ALU.subtract)
         nc.vector.tensor_tensor(flat(y01, every), flat(z0, every), flat(z1, every), ALU.add)
+        d2 = keep.tile([P, PACK, V], F32, name="d2", tag="r")
         nc.scalar.activation(flat(th2, every), flat(c2, every), ACT.Tanh, scale=0.5)
         for t in range(PACK):
             nc.vector.tensor_tensor(d2[:, t, :], feat[t][:].indirect(pos_sb[2][:]), y01[:, t, :], ALU.subtract)

@@ -67,7 +67,6 @@ def tile_picked_zrandla_relu_po_kernel(
                 )
             return codes, scales
 
-        offs_sb = load_list(offs, "offs_sb")
         xs_table = keep.tile([P, T], U8, name="xs_table")
         nc.vector.memset(xs_table[:].bitcast(I32), 0)
         w1_raw = [load_weight(w1[0:K_PASS, :], "w1_raw0")]
@@ -76,6 +75,7 @@ def tile_picked_zrandla_relu_po_kernel(
                 out=xs_table[32 * q : 32 * q + 4 * PASSES, :].bitcast(I32),
                 in_=x_scales.bitcast(I32)[:, 4 * q : 4 * q + 4, :],
             )
+        offs_sb = load_list(offs, "offs_sb")
         w1_raw.append(load_weight(w1[K_PASS:K, :], "w1_raw1"))
         xw_table = []
         for g in range(PASSES):
@@ -239,30 +239,44 @@ def tile_picked_zrandla_relu_po_kernel(
 
         weighted(0)
         nc.vector.scalar_tensor_tensor(flat(r, every), flat(a, every), 0.0, flat(b, every), ALU.max, ALU.subtract)
-        for t in range(1, PACK):
-            weighted(t)
+        weighted(1)
+        weighted(2)
+        nc.vector.tensor_tensor(flat(y01, pairs[0]), flat(z0, pairs[0]), flat(z1, pairs[0]), ALU.add)
+        weighted(3)
         nc.vector.tensor_tensor(flat(c2, every), flat(lg, every), flat(r, every), ALU.subtract)
-        nc.vector.tensor_tensor(flat(y01, every), flat(z0, every), flat(z1, every), ALU.add)
+        nc.vector.tensor_tensor(flat(y01, pairs[1]), flat(z0, pairs[1]), flat(z1, pairs[1]), ALU.add)
         d2 = keep.tile([P, PACK, V], F32, name="d2", tag="r")
         nc.scalar.activation(flat(th2, every), flat(c2, every), ACT.Tanh, scale=0.5)
-        for t in range(PACK):
-            nc.vector.tensor_tensor(d2[:, t, :], feat[t][:].indirect(pos_sb[2][:]), y01[:, t, :], ALU.subtract)
-
         o_codes = keep.tile([P, V], U32, name="o_codes", align_bytes=64)
         o_scales = keep.tile([P, V], U8, name="o_scales", align_bytes=64)
         out_rows = out_0.rearrange("(p t) v -> p t v", t=PACK)
         words_out = out_1[0].rearrange("p n t -> p (n t)").bitcast(I32)
         halves = [slice(0, V // 2), slice(V // 2, V)]
-        step = [keep.tile([P, PACK, V // 2], F32, name="step%d" % i) for i in range(2)]
-        res = [keep.tile([P, PACK, V // 2], F32, name="res%d" % i) for i in range(2)]
+        step, res = wide("step"), wide("res")
         res_bf = [keep.tile([P, V // 2, PACK], BF16, name="res_bf%d" % i, align_bytes=64) for i in range(2)]
-        for i, vs in enumerate(halves):
-            nc.vector.scalar_tensor_tensor(step[i][:], th2[:, :, vs], 1.0, d2[:, :, vs], ALU.add, ALU.mult)
-        for i, vs in enumerate(halves):
-            nc.vector.scalar_tensor_tensor(res[i][:], step[i][:], 0.5, y01[:, :, vs], ALU.mult, ALU.add)
-            nc.sync.dma_start(out=out_rows[:, :, vs], in_=res[i][:])
-        nc.scalar.copy(res_bf[0][:], res[0][:].rearrange("p t v -> p v t"))
-        nc.vector.tensor_copy(res_bf[1][:], res[1][:].rearrange("p t v -> p v t"))
+
+        def third(t):
+            nc.vector.tensor_tensor(d2[:, t, :], feat[t][:].indirect(pos_sb[2][:]), y01[:, t, :], ALU.subtract)
+
+        def make_step(ts, vs):
+            nc.vector.scalar_tensor_tensor(step[:, ts, vs], th2[:, ts, vs], 1.0, d2[:, ts, vs], ALU.add, ALU.mult)
+
+        def make_res(ts, vs):
+            nc.vector.scalar_tensor_tensor(res[:, ts, vs], step[:, ts, vs], 0.5, y01[:, ts, vs], ALU.mult, ALU.add)
+
+        for t in range(PACK - 1):
+            third(t)
+        make_step(pairs[0], slice(0, V))
+        third(PACK - 1)
+        make_res(pairs[0], slice(0, V))
+        nc.sync.dma_start(out=out_rows[:, pairs[0], :], in_=res[:, pairs[0], :])
+        for vs in halves:
+            make_step(pairs[1], vs)
+        for vs in halves:
+            make_res(pairs[1], vs)
+        nc.sync.dma_start(out=out_rows[:, pairs[1], :], in_=res[:, pairs[1], :])
+        nc.scalar.copy(res_bf[0][:], res[:, :, halves[0]].rearrange("p t v -> p v t"))
+        nc.vector.tensor_copy(res_bf[1][:], res[:, :, halves[1]].rearrange("p t v -> p v t"))
         for i, vs in enumerate(halves):
             nc.vector.quantize_mx(
                 out=o_codes[:, vs].bitcast(FP8X4),

@@ -1,6 +1,7 @@
 from contextlib import ExitStack
 
 import concourse.mybir as mybir
+from concourse.masks import make_identity
 
 K, T, S, V, H, N = 1024, 2048, 512, 256, 512, 512
 FLOPS = 2 * S * (K * H + 2 * H * N)
@@ -20,7 +21,13 @@ PACK = 4
 K_PASS = P * PACK
 PASSES = K // K_PASS
 QUADS = 4
+QUAD = P // QUADS
+SCALE_ROWS = 4
+LIST_ROWS = 16
 CHUNK = 128
+CHUNKS = S // CHUNK
+W1_SCALAR_COLS = 192
+WARM_PASSES = 2
 
 
 def tile_picked_zrandla_relu_po_kernel(
@@ -45,14 +52,12 @@ def tile_picked_zrandla_relu_po_kernel(
         def dealt_tile(name, tag):
             return keep.tile([P, PACK, P, PACK], BF16, name=name, tag=tag, align_bytes=64)
 
-        def deal(on_scalar, dealt, raw, first):
-            count = raw.shape[2] // PACK
-            dst = dealt[:, :, first : first + count, :].rearrange("p t m j -> p m t j")
-            src = raw.rearrange("p j (m t) -> p m t j", t=PACK)
-            if on_scalar:
-                nc.scalar.activation(dst, src, ACT.Copy)
-            else:
-                nc.vector.tensor_copy(dst, src)
+        def deal(copy, dealt, raw, first_col):
+            first, count = first_col // PACK, raw.shape[2] // PACK
+            copy(
+                dealt[:, :, first : first + count, :].rearrange("p t m j -> p m t j"),
+                raw.rearrange("p j (m t) -> p m t j", t=PACK),
+            )
 
         def quantise(dealt, name, pieces, tag):
             codes = keep.tile([P, K_PASS], U32, name=name + "_codes", tag=tag, align_bytes=64)
@@ -72,8 +77,8 @@ def tile_picked_zrandla_relu_po_kernel(
         w1_raw = [load_weight(w1[0:K_PASS, :], "w1_raw0")]
         for q in range(QUADS):
             nc.sync.dma_start(
-                out=xs_table[32 * q : 32 * q + 4 * PASSES, :].bitcast(I32),
-                in_=x_scales.bitcast(I32)[:, 4 * q : 4 * q + 4, :],
+                out=xs_table[QUAD * q : QUAD * q + SCALE_ROWS * PASSES, :].bitcast(I32),
+                in_=x_scales.bitcast(I32)[:, SCALE_ROWS * q : SCALE_ROWS * (q + 1), :],
             )
         offs_sb = load_list(offs, "offs_sb")
         w1_raw.append(load_weight(w1[K_PASS:K, :], "w1_raw1"))
@@ -84,50 +89,56 @@ def tile_picked_zrandla_relu_po_kernel(
                 out=table[:].bitcast(I32), in_=x_words[g].rearrange("p n t -> p (n t)").bitcast(I32)
             )
             xw_table.append(table)
-        w2_raw = [load_weight(w2[:, u * 256 : (u + 1) * 256], "w2_raw%d" % u) for u in range(2)]
+        w2_raw = [load_weight(w2[:, u * N // 2 : (u + 1) * N // 2], "w2_raw%d" % u) for u in range(2)]
         pos_sb = [load_list(src, "pos%d_sb" % d) for d, src in enumerate((pos1, pos2, pos3))]
         w3_raw = load_weight(w3, "w3_raw")
 
-        w1_q = []
+        ident = keep.tile([P, P], F32, name="ident")
+        make_identity(nc, ident[:])
+        preload = keep.tile([P, 1], F32, name="preload")
+        nc.scalar.activation(preload[:], ident[:, 0:1], ACT.Sigmoid)
+
         xs = keep.tile([P, S], U8, name="xs", align_bytes=64)
         nc.vector.tensor_copy(xs[:], xs_table[:].indirect(offs_sb[:]))
+        w1_q = []
         for g in range(PASSES):
             w1_dealt = dealt_tile("w1_dealt%d" % g, "w1_dealt%d" % g)
-            deal(True, w1_dealt, w1_raw[g][:, :, 0:192], 0)
-            deal(False, w1_dealt, w1_raw[g][:, :, 192:512], 48)
+            deal(nc.scalar.copy, w1_dealt, w1_raw[g][:, :, 0:W1_SCALAR_COLS], 0)
+            deal(nc.vector.tensor_copy, w1_dealt, w1_raw[g][:, :, W1_SCALAR_COLS:H], W1_SCALAR_COLS)
             w1_q.append(quantise(w1_dealt, "w1_%d" % g, 1, "w1_codes%d" % g))
         xw = [keep.tile([P, S], U32, name="xw%d" % g, align_bytes=64) for g in range(PASSES)]
         nc.vector.tensor_copy(xw[0][:], xw_table[0][:].indirect(offs_sb[:]))
-        for half in range(2):
+        for u in range(2):
+            entries = slice(u * S // 2, (u + 1) * S // 2)
             nc.vector.tensor_copy(
-                xw[1][:, 256 * half : 256 * (half + 1)],
-                xw_table[1][:].indirect(offs_sb[:, 16 * half : 16 * (half + 1)]),
+                xw[1][:, entries],
+                xw_table[1][:].indirect(offs_sb[:, entries.start // LIST_ROWS : entries.stop // LIST_ROWS]),
             )
 
         h_bf = keep.tile([P, S, PACK], BF16, name="h_bf", align_bytes=64)
         h_codes = keep.tile([P, S], U32, name="h_codes", align_bytes=64)
         h_scales = keep.tile([P, S], U8, name="h_scales", align_bytes=64)
-        banks = [hpsum.tile([P, PACK, CHUNK], F32, name="h_bank%d" % c) for c in range(S // CHUNK)]
+        h_banks = [hpsum.tile([P, PACK, CHUNK], F32, name="bank%d" % c) for c in range(CHUNKS)]
 
         def first_layer_pass(c, t, g):
             cols = slice(c * CHUNK, (c + 1) * CHUNK)
             chans = slice(t * P, (t + 1) * P)
             codes, scales = w1_q[g]
             nc.tensor.matmul_mx(
-                out=banks[c][:, t, :],
+                out=h_banks[c][:, t, :],
                 lhsT=codes[:, chans].bitcast(FP8X4),
                 lhsT_scale=scales[:, chans],
                 rhs=xw[g][:, cols].bitcast(FP8X4),
-                rhs_scale=xs[4 * g : P, cols],
+                rhs_scale=xs[SCALE_ROWS * g : P, cols],
                 start=(g == 0),
                 stop=(g == PASSES - 1),
             )
 
         w2_dealt = dealt_tile("w2_dealt", "w2_dealt")
-        for c in range(S // CHUNK):
+        for c in range(CHUNKS):
             first_layer_pass(c, 0, 0)
         warm = mpsum.tile([P, S], F32, name="acc")
-        for t in range(1, 3):
+        for t in range(1, 1 + WARM_PASSES):
             nc.tensor.matmul_mx(
                 out=warm[:],
                 lhsT=w1_q[0][0][:, t * P : (t + 1) * P].bitcast(FP8X4),
@@ -137,23 +148,22 @@ def tile_picked_zrandla_relu_po_kernel(
                 start=True,
                 stop=True,
             )
-        for c in range(S // CHUNK):
+        for c in range(CHUNKS):
             cols = slice(c * CHUNK, (c + 1) * CHUNK)
-            bank = banks[c]
             first_layer_pass(c, 0, 1)
             for t in range(1, PACK):
                 for g in range(PASSES):
                     first_layer_pass(c, t, g)
-            if c < 2:
-                deal(False, w2_dealt, w2_raw[c][:], 64 * c)
-            nc.scalar.activation(h_bf[:, cols, :], bank[:].rearrange("p t n -> p n t"), ACT.Relu)
+            if c < len(w2_raw):
+                deal(nc.vector.tensor_copy, w2_dealt, w2_raw[c][:], c * N // 2)
+            nc.scalar.activation(h_bf[:, cols, :], h_banks[c][:].rearrange("p t n -> p n t"), ACT.Relu)
             nc.vector.quantize_mx(
                 out=h_codes[:, cols].bitcast(FP8X4),
                 scales=h_scales[:, cols],
                 in_=h_bf[:, cols, :].rearrange("p n t -> p (n t)"),
             )
 
-        def product(acc, w_q, t, cols):
+        def second_layer_pass(acc, w_q, t, cols):
             codes, scales = w_q
             chans = slice(t * P, (t + 1) * P)
             nc.tensor.matmul_mx(
@@ -166,18 +176,15 @@ def tile_picked_zrandla_relu_po_kernel(
                 stop=True,
             )
 
-        def to_sbuf(acc, name, on_scalar):
+        def scalar_to_sbuf(acc, name, sign):
             row = keep.tile([P, S], F32, name=name)
-            if on_scalar:
-                nc.scalar.copy(row[:], acc[:])
-            else:
-                nc.vector.tensor_copy(row[:], acc[:])
+            nc.scalar.activation(row[:], acc[:], ACT.Copy, scale=sign)
             return row
 
-        def second_layer(w_q, t, name):
+        def second_layer(w_q, t, name, sign):
             acc = mpsum.tile([P, S], F32, name="acc")
-            product(acc, w_q, t, slice(0, S))
-            return to_sbuf(acc, name, True)
+            second_layer_pass(acc, w_q, t, slice(0, S))
+            return scalar_to_sbuf(acc, name, sign)
 
         def wide(name):
             return keep.tile([P, PACK, V], F32, name=name)
@@ -187,93 +194,118 @@ def tile_picked_zrandla_relu_po_kernel(
 
         w2_q = quantise(w2_dealt, "w2", PACK, "reused")
         early = [mpsum.tile([P, S], F32, name="acc") for t in range(2)]
-        for cols in (slice(0, 256), slice(256, 384), slice(384, 512)):
+        for cols in (slice(0, 2 * CHUNK), slice(2 * CHUNK, 3 * CHUNK), slice(3 * CHUNK, S)):
             for t in range(2):
-                product(early[t], w2_q, t, cols)
-        score = [to_sbuf(early[t], "score%d" % t, t > 0) for t in range(2)]
-        score = score + [second_layer(w2_q, t, "score%d" % t) for t in range(2, PACK)]
+                second_layer_pass(early[t], w2_q, t, cols)
+        neg_score = [keep.tile([P, S], F32, name="neg_score0")]
+        nc.vector.tensor_scalar(neg_score[0][:], early[0][:], -1.0, None, ALU.mult)
+        neg_score.append(scalar_to_sbuf(early[1], "neg_score1", -1.0))
+        for t in range(2, PACK):
+            neg_score.append(second_layer(w2_q, t, "neg_score%d" % t, -1.0))
         w3_dealt = dealt_tile("w3_dealt", "reused")
-        deal(True, w3_dealt, w3_raw[:], 0)
+        deal(nc.scalar.copy, w3_dealt, w3_raw[:], 0)
 
-        s0, a = wide("s0"), wide("a")
-        th = keep.tile([P, PACK, V], F32, name="th", tag="w3_raw")
-        q1, q0, lg = wide("q1"), wide("q0"), wide("lg")
-        pairs = (slice(0, 2), slice(2, 4))
+        neg_s0, neg_a = wide("neg_s0"), wide("neg_a")
+        q01 = keep.tile([P, 2, PACK, V], F32, name="q01", tag="w3_raw")
+        q0, q1 = q01[:, 0, :, :], q01[:, 1, :, :]
+        log_q = wide("log_q")
+        pairs = (slice(0, 2), slice(2, PACK))
         every = slice(0, PACK)
 
-        def pair_weights(ts):
-            nc.scalar.activation(flat(th, ts), flat(a, ts), ACT.Tanh, scale=0.5)
-            nc.scalar.activation(flat(q0, ts), flat(th, ts), ACT.Copy, scale=-0.5, bias=0.5)
-            nc.scalar.activation(flat(q1, ts), flat(th, ts), ACT.Copy, scale=0.5, bias=0.5)
+        def gather_first(t):
+            nc.vector.tensor_copy(neg_s0[:, t, :], neg_score[t][:].indirect(pos_sb[0][:]))
 
-        def first(t):
-            nc.vector.tensor_copy(s0[:, t, :], score[t][:].indirect(pos_sb[0][:]))
+        def gather_difference(dst, t, d):
+            nc.vector.tensor_tensor(
+                dst[:, t, :], neg_score[t][:].indirect(pos_sb[d][:]), neg_s0[:, t, :], ALU.subtract
+            )
 
-        def difference(dst, t, d):
-            nc.vector.tensor_tensor(dst[:, t, :], score[t][:].indirect(pos_sb[d][:]), s0[:, t, :], ALU.subtract)
-
-        first(0)
+        gather_first(0)
         for t in range(PACK):
             if t + 1 < PACK:
-                first(t + 1)
-            difference(a, t, 1)
+                gather_first(t + 1)
+            gather_difference(neg_a, t, 1)
         w3_q = quantise(w3_dealt, "w3", 1, "w3_codes")
-        b = keep.tile([P, PACK, V], F32, name="b", tag="reused", align_bytes=64)
+        neg_b = keep.tile([P, PACK, V], F32, name="neg_b", tag="reused", align_bytes=64)
         for t in range(PACK):
-            difference(b, t, 2)
+            gather_difference(neg_b, t, 2)
         feat = []
         for ts in pairs:
-            pair_weights(ts)
-            feat = feat + [second_layer(w3_q, t, "feat%d" % t) for t in range(ts.start, ts.stop)]
+            nc.scalar.activation(flat(q1, ts), flat(neg_a, ts), ACT.Sigmoid, scale=-1.0)
+            nc.scalar.activation(flat(q0, ts), flat(neg_a, ts), ACT.Sigmoid)
+            for t in range(ts.start, ts.stop):
+                feat.append(second_layer(w3_q, t, "feat%d" % t, 1.0))
 
         mag = wide("mag")
-        nc.scalar.activation(flat(mag, every), flat(th, every), ACT.Abs)
-        nc.scalar.activation(flat(lg, every), flat(mag, every), ACT.Ln, scale=0.5, bias=0.5)
+        nc.scalar.activation(flat(mag, every), flat(q1, every), ACT.Abs, bias=-0.5)
+        for ts in pairs:
+            nc.scalar.activation(flat(log_q, ts), flat(mag, ts), ACT.Ln, bias=0.5)
 
-        z0, z1, y01, c2, th2 = (wide(n) for n in ("z0", "z1", "y01", "c2", "th2"))
-        r = keep.tile([P, PACK, V], F32, name="r", tag="r")
+        z0, z1, y01, excess, d2 = (wide(name) for name in ("z0", "z1", "y01", "excess", "d2"))
 
-        def weighted(t):
+        def gather_weighted(t):
             nc.vector.tensor_tensor(z0[:, t, :], feat[t][:].indirect(pos_sb[0][:]), q0[:, t, :], ALU.mult)
             nc.vector.tensor_tensor(z1[:, t, :], feat[t][:].indirect(pos_sb[1][:]), q1[:, t, :], ALU.mult)
 
-        weighted(0)
-        nc.vector.scalar_tensor_tensor(flat(r, every), flat(a, every), 0.0, flat(b, every), ALU.max, ALU.subtract)
-        weighted(1)
-        weighted(2)
-        nc.vector.tensor_tensor(flat(y01, pairs[0]), flat(z0, pairs[0]), flat(z1, pairs[0]), ALU.add)
-        weighted(3)
-        nc.vector.tensor_tensor(flat(c2, every), flat(lg, every), flat(r, every), ALU.subtract)
-        nc.vector.tensor_tensor(flat(y01, pairs[1]), flat(z0, pairs[1]), flat(z1, pairs[1]), ALU.add)
-        d2 = keep.tile([P, PACK, V], F32, name="d2", tag="r")
-        nc.scalar.activation(flat(th2, every), flat(c2, every), ACT.Tanh, scale=0.5)
+        def add_pair(ts):
+            nc.vector.tensor_tensor(flat(y01, ts), flat(z0, ts), flat(z1, ts), ALU.add)
+
+        gather_weighted(0)
+        nc.vector.scalar_tensor_tensor(
+            flat(excess, every), flat(neg_a, every), 0.0, flat(neg_b, every), ALU.min, ALU.subtract
+        )
+        gather_weighted(1)
+        gather_weighted(2)
+        add_pair(pairs[0])
+        gather_weighted(3)
+        add_pair(pairs[1])
+
+        def block(tile, ts, i):
+            return flat(tile, ts)[:, i * P : (i + 1) * P]
+
+        blocks = 2 * V // P
+        sums = [hpsum.tile([P, blocks, P], F32, name="bank%d" % u) for u in range(2)]
+        for u, ts in enumerate(pairs):
+            for i in range(blocks):
+                for src, last in ((excess, False), (log_q, True)):
+                    nc.tensor.matmul(
+                        sums[u][:, i, :], block(src, ts, i), ident[:], start=not last, stop=last, is_transpose=True
+                    )
+        q2 = []
+        for u in range(2):
+            turned = keep.tile([P, blocks, P], F32, name="turned%d" % u)
+            nc.scalar.activation(turned[:], sums[u][:], ACT.Sigmoid)
+            back = hpsum.tile([P, 2, V], F32, name="bank%d" % (2 + u))
+            for i in range(blocks):
+                nc.tensor.transpose(block(back, slice(0, 2), i), turned[:, i, :], ident[:])
+            q2.append(back)
+
         o_codes = keep.tile([P, V], U32, name="o_codes", align_bytes=64)
         o_scales = keep.tile([P, V], U8, name="o_scales", align_bytes=64)
         out_rows = out_0.rearrange("(p t) v -> p t v", t=PACK)
-        words_out = out_1[0].rearrange("p n t -> p (n t)").bitcast(I32)
         halves = [slice(0, V // 2), slice(V // 2, V)]
         step, res = wide("step"), wide("res")
         res_bf = [keep.tile([P, V // 2, PACK], BF16, name="res_bf%d" % i, align_bytes=64) for i in range(2)]
 
-        def third(t):
+        def gather_third(t):
             nc.vector.tensor_tensor(d2[:, t, :], feat[t][:].indirect(pos_sb[2][:]), y01[:, t, :], ALU.subtract)
 
-        def make_step(ts, vs):
-            nc.vector.scalar_tensor_tensor(step[:, ts, vs], th2[:, ts, vs], 1.0, d2[:, ts, vs], ALU.add, ALU.mult)
+        def make_step(u, vs):
+            nc.vector.tensor_tensor(step[:, pairs[u], vs], q2[u][:, :, vs], d2[:, pairs[u], vs], ALU.mult)
 
-        def make_res(ts, vs):
-            nc.vector.scalar_tensor_tensor(res[:, ts, vs], step[:, ts, vs], 0.5, y01[:, ts, vs], ALU.mult, ALU.add)
+        def make_res(u, vs):
+            nc.vector.tensor_tensor(res[:, pairs[u], vs], step[:, pairs[u], vs], y01[:, pairs[u], vs], ALU.add)
 
         for t in range(PACK - 1):
-            third(t)
-        make_step(pairs[0], slice(0, V))
-        third(PACK - 1)
-        make_res(pairs[0], slice(0, V))
+            gather_third(t)
+        make_step(0, slice(0, V))
+        gather_third(PACK - 1)
+        make_res(0, slice(0, V))
         nc.sync.dma_start(out=out_rows[:, pairs[0], :], in_=res[:, pairs[0], :])
         for vs in halves:
-            make_step(pairs[1], vs)
+            make_step(1, vs)
         for vs in halves:
-            make_res(pairs[1], vs)
+            make_res(1, vs)
         nc.sync.dma_start(out=out_rows[:, pairs[1], :], in_=res[:, pairs[1], :])
         nc.scalar.copy(res_bf[0][:], res[:, :, halves[0]].rearrange("p t v -> p v t"))
         nc.vector.tensor_copy(res_bf[1][:], res[:, :, halves[1]].rearrange("p t v -> p v t"))
@@ -283,9 +315,10 @@ def tile_picked_zrandla_relu_po_kernel(
                 scales=o_scales[:, vs],
                 in_=res_bf[i][:].rearrange("p v t -> p (v t)"),
             )
-        nc.sync.dma_start(out=words_out, in_=o_codes[:].bitcast(I32))
+        nc.sync.dma_start(out=out_1[0].rearrange("p n t -> p (n t)").bitcast(I32), in_=o_codes[:].bitcast(I32))
         for q in range(QUADS):
             queue = nc.scalar if q % 2 else nc.sync
             queue.dma_start(
-                out=out_2[0].bitcast(I32)[4 * q : 4 * q + 4, :], in_=o_scales[32 * q : 32 * q + 4, :].bitcast(I32)
+                out=out_2[0].bitcast(I32)[SCALE_ROWS * q : SCALE_ROWS * (q + 1), :],
+                in_=o_scales[QUAD * q : QUAD * q + SCALE_ROWS, :].bitcast(I32),
             )

@@ -27,7 +27,6 @@ LIST_ROWS = 16
 CHUNK = 128
 CHUNKS = S // CHUNK
 W1_SCALAR_COLS = 192
-WARM_PASSES = 2
 
 
 def tile_picked_zrandla_relu_po_kernel(
@@ -36,8 +35,10 @@ def tile_picked_zrandla_relu_po_kernel(
     nc = tc.nc
     with ExitStack() as ctx:
         keep = ctx.enter_context(tc.tile_pool(name="keep", bufs=1))
-        hpsum = ctx.enter_context(tc.psum_pool(name="hpsum", bufs=1))
-        mpsum = ctx.enter_context(tc.psum_pool(name="mpsum", bufs=4))
+        psum = ctx.enter_context(tc.psum_pool(name="psum", bufs=1))
+
+        def bank(index, shape):
+            return psum.tile(shape, F32, name="bank%d" % index)
 
         def load_list(src, name):
             tile = keep.tile(list(src.shape), U16, name=name)
@@ -81,9 +82,10 @@ def tile_picked_zrandla_relu_po_kernel(
                 in_=x_scales.bitcast(I32)[:, SCALE_ROWS * q : SCALE_ROWS * (q + 1), :],
             )
         offs_sb = load_list(offs, "offs_sb")
-        w1_raw.append(load_weight(w1[K_PASS:K, :], "w1_raw1"))
         xw_table = []
         for g in range(PASSES):
+            if g == 1:
+                w1_raw.append(load_weight(w1[K_PASS:K, :], "w1_raw1"))
             table = keep.tile([P, T], U32, name="xw_table%d" % g)
             nc.sync.dma_start(
                 out=table[:].bitcast(I32), in_=x_words[g].rearrange("p n t -> p (n t)").bitcast(I32)
@@ -101,13 +103,14 @@ def tile_picked_zrandla_relu_po_kernel(
         xs = keep.tile([P, S], U8, name="xs", align_bytes=64)
         nc.vector.tensor_copy(xs[:], xs_table[:].indirect(offs_sb[:]))
         w1_q = []
+        xw = [keep.tile([P, S], U32, name="xw%d" % g, align_bytes=64) for g in range(PASSES)]
         for g in range(PASSES):
+            if g == 1:
+                nc.vector.tensor_copy(xw[0][:], xw_table[0][:].indirect(offs_sb[:]))
             w1_dealt = dealt_tile("w1_dealt%d" % g, "w1_dealt%d" % g)
             deal(nc.scalar.copy, w1_dealt, w1_raw[g][:, :, 0:W1_SCALAR_COLS], 0)
             deal(nc.vector.tensor_copy, w1_dealt, w1_raw[g][:, :, W1_SCALAR_COLS:H], W1_SCALAR_COLS)
             w1_q.append(quantise(w1_dealt, "w1_%d" % g, 1, "w1_codes%d" % g))
-        xw = [keep.tile([P, S], U32, name="xw%d" % g, align_bytes=64) for g in range(PASSES)]
-        nc.vector.tensor_copy(xw[0][:], xw_table[0][:].indirect(offs_sb[:]))
         for u in range(2):
             entries = slice(u * S // 2, (u + 1) * S // 2)
             nc.vector.tensor_copy(
@@ -118,7 +121,7 @@ def tile_picked_zrandla_relu_po_kernel(
         h_bf = keep.tile([P, S, PACK], BF16, name="h_bf", align_bytes=64)
         h_codes = keep.tile([P, S], U32, name="h_codes", align_bytes=64)
         h_scales = keep.tile([P, S], U8, name="h_scales", align_bytes=64)
-        h_banks = [hpsum.tile([P, PACK, CHUNK], F32, name="bank%d" % c) for c in range(CHUNKS)]
+        h_banks = [bank(c, [P, PACK, CHUNK]) for c in range(CHUNKS)]
 
         def first_layer_pass(c, t, g):
             cols = slice(c * CHUNK, (c + 1) * CHUNK)
@@ -130,30 +133,30 @@ def tile_picked_zrandla_relu_po_kernel(
                 lhsT_scale=scales[:, chans],
                 rhs=xw[g][:, cols].bitcast(FP8X4),
                 rhs_scale=xs[SCALE_ROWS * g : P, cols],
-                start=(g == 0),
-                stop=(g == PASSES - 1),
+                start=(g == 0 and t == 0),
+                stop=(g == PASSES - 1 and t == PACK - 1),
             )
 
+        for g in range(PASSES):
+            for c in range(CHUNKS):
+                for t in range(PACK):
+                    first_layer_pass(c, t, g)
+
         w2_dealt = dealt_tile("w2_dealt", "w2_dealt")
-        for c in range(CHUNKS):
-            first_layer_pass(c, 0, 0)
-        warm = mpsum.tile([P, S], F32, name="acc")
-        for t in range(1, 1 + WARM_PASSES):
-            nc.tensor.matmul_mx(
-                out=warm[:],
-                lhsT=w1_q[0][0][:, t * P : (t + 1) * P].bitcast(FP8X4),
-                lhsT_scale=w1_q[0][1][:, t * P : (t + 1) * P],
-                rhs=xw[0][:].bitcast(FP8X4),
-                rhs_scale=xs[:],
-                start=True,
-                stop=True,
+        w2_codes = keep.tile([P, K_PASS], U32, name="w2_codes", tag="reused", align_bytes=64)
+        w2_scales = keep.tile([P, K_PASS], U8, name="w2_scales", align_bytes=64)
+        w2_q = (w2_codes, w2_scales)
+
+        def quantise_w2(t):
+            chans = slice(t * P, (t + 1) * P)
+            nc.vector.quantize_mx(
+                out=w2_codes[:, chans].bitcast(FP8X4),
+                scales=w2_scales[:, chans],
+                in_=w2_dealt[:, t, :, :].rearrange("p m j -> p (m j)"),
             )
+
         for c in range(CHUNKS):
             cols = slice(c * CHUNK, (c + 1) * CHUNK)
-            first_layer_pass(c, 0, 1)
-            for t in range(1, PACK):
-                for g in range(PASSES):
-                    first_layer_pass(c, t, g)
             if c < len(w2_raw):
                 deal(nc.vector.tensor_copy, w2_dealt, w2_raw[c][:], c * N // 2)
             nc.scalar.activation(h_bf[:, cols, :], h_banks[c][:].rearrange("p t n -> p n t"), ACT.Relu)
@@ -162,12 +165,15 @@ def tile_picked_zrandla_relu_po_kernel(
                 scales=h_scales[:, cols],
                 in_=h_bf[:, cols, :].rearrange("p n t -> p (n t)"),
             )
+            if c == len(w2_raw) - 1:
+                quantise_w2(0)
+        quantise_w2(1)
 
         def second_layer_pass(acc, w_q, t, cols):
             codes, scales = w_q
             chans = slice(t * P, (t + 1) * P)
             nc.tensor.matmul_mx(
-                out=acc[:, cols],
+                out=acc,
                 lhsT=codes[:, chans].bitcast(FP8X4),
                 lhsT_scale=scales[:, chans],
                 rhs=h_codes[:, cols].bitcast(FP8X4),
@@ -176,15 +182,12 @@ def tile_picked_zrandla_relu_po_kernel(
                 stop=True,
             )
 
-        def scalar_to_sbuf(acc, name, sign):
+        def second_layer(w_q, t, name, index):
+            acc = bank(index, [P, S])
+            second_layer_pass(acc[:], w_q, t, slice(0, S))
             row = keep.tile([P, S], F32, name=name)
-            nc.scalar.activation(row[:], acc[:], ACT.Copy, scale=sign)
+            nc.scalar.copy(row[:], acc[:])
             return row
-
-        def second_layer(w_q, t, name, sign):
-            acc = mpsum.tile([P, S], F32, name="acc")
-            second_layer_pass(acc, w_q, t, slice(0, S))
-            return scalar_to_sbuf(acc, name, sign)
 
         def wide(name):
             return keep.tile([P, PACK, V], F32, name=name)
@@ -192,124 +195,115 @@ def tile_picked_zrandla_relu_po_kernel(
         def flat(tile, ts):
             return tile[:, ts, :].rearrange("p t v -> p (t v)")
 
-        w2_q = quantise(w2_dealt, "w2", PACK, "reused")
-        early = [mpsum.tile([P, S], F32, name="acc") for t in range(2)]
-        for cols in (slice(0, 2 * CHUNK), slice(2 * CHUNK, 3 * CHUNK), slice(3 * CHUNK, S)):
-            for t in range(2):
-                second_layer_pass(early[t], w2_q, t, cols)
-        neg_score = [keep.tile([P, S], F32, name="neg_score0")]
-        nc.vector.tensor_scalar(neg_score[0][:], early[0][:], -1.0, None, ALU.mult)
-        neg_score.append(scalar_to_sbuf(early[1], "neg_score1", -1.0))
+        most, last = slice(0, S - CHUNK), slice(S - CHUNK, S)
+        acc_most, acc_last, acc_1 = bank(4, [P, S - CHUNK]), bank(5, [P, CHUNK]), bank(6, [P, S])
+        for cols in (slice(0, 2 * CHUNK), slice(2 * CHUNK, 3 * CHUNK)):
+            second_layer_pass(acc_most[:, cols], w2_q, 0, cols)
+        second_layer_pass(acc_last[:], w2_q, 0, last)
+        second_layer_pass(acc_1[:], w2_q, 1, slice(0, S))
+        score = [keep.tile([P, S], F32, name="score%d" % t) for t in range(2)]
+        nc.scalar.copy(score[0][:, most], acc_most[:])
+        nc.vector.tensor_copy(score[0][:, last], acc_last[:])
+        nc.scalar.copy(score[1][:], acc_1[:])
         for t in range(2, PACK):
-            neg_score.append(second_layer(w2_q, t, "neg_score%d" % t, -1.0))
+            quantise_w2(t)
+        score.append(second_layer(w2_q, 2, "score2", 7))
+        score.append(second_layer(w2_q, 3, "score3", 0))
         w3_dealt = dealt_tile("w3_dealt", "reused")
         deal(nc.scalar.copy, w3_dealt, w3_raw[:], 0)
 
-        neg_s0, neg_a = wide("neg_s0"), wide("neg_a")
+        s0, a = wide("s0"), wide("a")
         q01 = keep.tile([P, 2, PACK, V], F32, name="q01", tag="w3_raw")
         q0, q1 = q01[:, 0, :, :], q01[:, 1, :, :]
-        log_q = wide("log_q")
         pairs = (slice(0, 2), slice(2, PACK))
         every = slice(0, PACK)
 
         def gather_first(t):
-            nc.vector.tensor_copy(neg_s0[:, t, :], neg_score[t][:].indirect(pos_sb[0][:]))
+            nc.vector.tensor_copy(s0[:, t, :], score[t][:].indirect(pos_sb[0][:]))
 
         def gather_difference(dst, t, d):
-            nc.vector.tensor_tensor(
-                dst[:, t, :], neg_score[t][:].indirect(pos_sb[d][:]), neg_s0[:, t, :], ALU.subtract
-            )
+            nc.vector.tensor_tensor(dst[:, t, :], score[t][:].indirect(pos_sb[d][:]), s0[:, t, :], ALU.subtract)
 
         gather_first(0)
         for t in range(PACK):
             if t + 1 < PACK:
                 gather_first(t + 1)
-            gather_difference(neg_a, t, 1)
+            gather_difference(a, t, 1)
         w3_q = quantise(w3_dealt, "w3", 1, "w3_codes")
-        neg_b = keep.tile([P, PACK, V], F32, name="neg_b", tag="reused", align_bytes=64)
+        b = keep.tile([P, PACK, V], F32, name="b", tag="reused", align_bytes=64)
         for t in range(PACK):
-            gather_difference(neg_b, t, 2)
+            gather_difference(b, t, 2)
+        neg_relu = wide("neg_relu")
+        nc.vector.tensor_scalar(flat(neg_relu, every), flat(a, every), -1.0, 0.0, ALU.mult, ALU.min)
         feat = []
         for ts in pairs:
-            nc.scalar.activation(flat(q1, ts), flat(neg_a, ts), ACT.Sigmoid, scale=-1.0)
-            nc.scalar.activation(flat(q0, ts), flat(neg_a, ts), ACT.Sigmoid)
+            nc.scalar.activation(flat(q1, ts), flat(a, ts), ACT.Sigmoid)
+            nc.scalar.activation(flat(q0, ts), flat(a, ts), ACT.Sigmoid, scale=-1.0)
             for t in range(ts.start, ts.stop):
-                feat.append(second_layer(w3_q, t, "feat%d" % t, 1.0))
+                feat.append(second_layer(w3_q, t, "feat%d" % t, 1 + t))
 
-        mag = wide("mag")
+        mag, log_q = wide("mag"), wide("log_q")
         nc.scalar.activation(flat(mag, every), flat(q1, every), ACT.Abs, bias=-0.5)
         for ts in pairs:
             nc.scalar.activation(flat(log_q, ts), flat(mag, ts), ACT.Ln, bias=0.5)
 
-        z0, z1, y01, excess, d2 = (wide(name) for name in ("z0", "z1", "y01", "excess", "d2"))
-
-        def gather_weighted(t):
-            nc.vector.tensor_tensor(z0[:, t, :], feat[t][:].indirect(pos_sb[0][:]), q0[:, t, :], ALU.mult)
-            nc.vector.tensor_tensor(z1[:, t, :], feat[t][:].indirect(pos_sb[1][:]), q1[:, t, :], ALU.mult)
-
-        def add_pair(ts):
-            nc.vector.tensor_tensor(flat(y01, ts), flat(z0, ts), flat(z1, ts), ALU.add)
-
-        gather_weighted(0)
-        nc.vector.scalar_tensor_tensor(
-            flat(excess, every), flat(neg_a, every), 0.0, flat(neg_b, every), ALU.min, ALU.subtract
-        )
-        gather_weighted(1)
-        gather_weighted(2)
-        add_pair(pairs[0])
-        gather_weighted(3)
-        add_pair(pairs[1])
-
-        def block(tile, ts, i):
-            return flat(tile, ts)[:, i * P : (i + 1) * P]
-
-        blocks = 2 * V // P
-        sums = [hpsum.tile([P, blocks, P], F32, name="bank%d" % u) for u in range(2)]
-        for u, ts in enumerate(pairs):
-            for i in range(blocks):
-                for src, last in ((excess, False), (log_q, True)):
+        def add_turned(acc, terms):
+            blocks = acc.shape[1]
+            for n, term in enumerate(terms):
+                for i in range(blocks):
                     nc.tensor.matmul(
-                        sums[u][:, i, :], block(src, ts, i), ident[:], start=not last, stop=last, is_transpose=True
+                        acc[:, i, :],
+                        term[:, i * P : (i + 1) * P],
+                        ident[:],
+                        start=(n == 0 and i == 0),
+                        stop=(n == len(terms) - 1 and i == blocks - 1),
+                        is_transpose=True,
                     )
-        q2 = []
-        for u in range(2):
-            turned = keep.tile([P, blocks, P], F32, name="turned%d" % u)
-            nc.scalar.activation(turned[:], sums[u][:], ACT.Sigmoid)
-            back = hpsum.tile([P, 2, V], F32, name="bank%d" % (2 + u))
-            for i in range(blocks):
-                nc.tensor.transpose(block(back, slice(0, 2), i), turned[:, i, :], ident[:])
-            q2.append(back)
+
+        halves = V // P
+        keep01 = []
+        for u, ts in enumerate(pairs):
+            c_turned = bank(5 + u, [P, 2 * halves, P])
+            add_turned(c_turned, [flat(term, ts) for term in (b, neg_relu, log_q)])
+            weight = keep.tile([P, 2 * halves, P], F32, name="keep01_%d" % u)
+            nc.scalar.activation(weight[:], c_turned[:], ACT.Sigmoid, scale=-1.0)
+            keep01.append(weight)
+
+        minus = keep.tile([P, V], F32, name="minus")
+        nc.gpsimd.memset(minus[:], -1.0)
+        neg_y2, z1, res = (wide(name) for name in ("neg_y2", "z1", "res"))
+        z0 = [keep.tile([P, 2, V], F32, name=name) for name in ("z0", "log_q")]
+        diff = []
+        for t in range(PACK):
+            terms = (z0[t // 2][:, t % 2, :], neg_y2[:, t, :], z1[:, t, :])
+            for dst, d, factor in zip(terms, (0, 2, 1), (q0[:, t, :], minus[:], q1[:, t, :])):
+                nc.vector.tensor_tensor(dst, feat[t][:].indirect(pos_sb[d][:]), factor, ALU.mult)
+            acc = bank((7 + t) % 8, [P, halves, P])
+            add_turned(acc, terms)
+            diff.append(acc)
+
+        back = []
+        for t in range(PACK):
+            step = keep.tile([P, halves, P], F32, name="step%d" % t)
+            first = (t % 2) * halves
+            nc.vector.tensor_tensor(step[:], diff[t][:], keep01[t // 2][:, first : first + halves, :], ALU.mult)
+            acc = bank(3 + t, [P, V])
+            for i in range(halves):
+                nc.tensor.transpose(acc[:, i * P : (i + 1) * P], step[:, i, :], ident[:])
+            back.append(acc)
+        out_rows = out_0.rearrange("(p t) v -> p t v", t=PACK)
+        for t in range(PACK):
+            nc.vector.tensor_tensor(res[:, t, :], back[t][:], neg_y2[:, t, :], ALU.subtract)
+            if t % 2:
+                nc.sync.dma_start(out=out_rows[:, pairs[t // 2], :], in_=res[:, pairs[t // 2], :])
 
         o_codes = keep.tile([P, V], U32, name="o_codes", align_bytes=64)
         o_scales = keep.tile([P, V], U8, name="o_scales", align_bytes=64)
-        out_rows = out_0.rearrange("(p t) v -> p t v", t=PACK)
-        halves = [slice(0, V // 2), slice(V // 2, V)]
-        step, res = wide("step"), wide("res")
+        centres = [slice(0, V // 2), slice(V // 2, V)]
         res_bf = [keep.tile([P, V // 2, PACK], BF16, name="res_bf%d" % i, align_bytes=64) for i in range(2)]
-
-        def gather_third(t):
-            nc.vector.tensor_tensor(d2[:, t, :], feat[t][:].indirect(pos_sb[2][:]), y01[:, t, :], ALU.subtract)
-
-        def make_step(u, vs):
-            nc.vector.tensor_tensor(step[:, pairs[u], vs], q2[u][:, :, vs], d2[:, pairs[u], vs], ALU.mult)
-
-        def make_res(u, vs):
-            nc.vector.tensor_tensor(res[:, pairs[u], vs], step[:, pairs[u], vs], y01[:, pairs[u], vs], ALU.add)
-
-        for t in range(PACK - 1):
-            gather_third(t)
-        make_step(0, slice(0, V))
-        gather_third(PACK - 1)
-        make_res(0, slice(0, V))
-        nc.sync.dma_start(out=out_rows[:, pairs[0], :], in_=res[:, pairs[0], :])
-        for vs in halves:
-            make_step(1, vs)
-        for vs in halves:
-            make_res(1, vs)
-        nc.sync.dma_start(out=out_rows[:, pairs[1], :], in_=res[:, pairs[1], :])
-        nc.scalar.copy(res_bf[0][:], res[:, :, halves[0]].rearrange("p t v -> p v t"))
-        nc.vector.tensor_copy(res_bf[1][:], res[:, :, halves[1]].rearrange("p t v -> p v t"))
-        for i, vs in enumerate(halves):
+        nc.scalar.copy(res_bf[1][:], res[:, :, centres[1]].rearrange("p t v -> p v t"))
+        nc.vector.tensor_copy(res_bf[0][:], res[:, :, centres[0]].rearrange("p t v -> p v t"))
+        for i, vs in enumerate(centres):
             nc.vector.quantize_mx(
                 out=o_codes[:, vs].bitcast(FP8X4),
                 scales=o_scales[:, vs],

@@ -230,22 +230,21 @@ def tile_picked_zrandla_relu_po_kernel(
                 gather_first(t + 1)
             gather_difference(a, t, 1)
         w3_q = quantise(w3_dealt, "w3", 1, "w3_codes")
-        b = keep.tile([P, PACK, V], F32, name="b", tag="reused", align_bytes=64)
+        b_relu = keep.tile([P, 2, PACK, V], F32, name="b_relu", tag="reused", align_bytes=64)
+        b, neg_relu = b_relu[:, 0, :, :], b_relu[:, 1, :, :]
         for t in range(PACK):
             gather_difference(b, t, 2)
-        neg_relu = wide("neg_relu")
         nc.vector.tensor_scalar(flat(neg_relu, every), flat(a, every), -1.0, 0.0, ALU.mult, ALU.min)
-        feat = []
         for ts in pairs:
             nc.scalar.activation(flat(q1, ts), flat(a, ts), ACT.Sigmoid)
             nc.scalar.activation(flat(q0, ts), flat(a, ts), ACT.Sigmoid, scale=-1.0)
-            for t in range(ts.start, ts.stop):
-                feat.append(second_layer(w3_q, t, "feat%d" % t, 1 + t))
 
         mag, log_q = wide("mag"), wide("log_q")
         nc.scalar.activation(flat(mag, every), flat(q1, every), ACT.Abs, bias=-0.5)
+        feat = [second_layer(w3_q, t, "feat%d" % t, 1 + t) for t in range(2)]
         for ts in pairs:
             nc.scalar.activation(flat(log_q, ts), flat(mag, ts), ACT.Ln, bias=0.5)
+        feat.extend(second_layer(w3_q, t, "feat%d" % t, 1 + t) for t in range(2, PACK))
 
         def add_turned(acc, terms):
             blocks = acc.shape[1]

@@ -46,7 +46,7 @@ def tile_picked_zrandla_relu_po_kernel(
             return tile
 
         def load_weight(rows, name):
-            raw = keep.tile([P, PACK, rows.shape[1]], F32, name=name, tag=name)
+            raw = keep.tile([P, PACK, rows.shape[1]], F32, name=name, tag=name, align_bytes=64)
             nc.sync.dma_start(out=raw[:], in_=rows.rearrange("(p j) c -> p j c", j=PACK))
             return raw
 
@@ -56,8 +56,8 @@ def tile_picked_zrandla_relu_po_kernel(
         def deal(copy, dealt, raw, first_col):
             first, count = first_col // PACK, raw.shape[2] // PACK
             copy(
-                dealt[:, :, first : first + count, :].rearrange("p t m j -> p m t j"),
-                raw.rearrange("p j (m t) -> p m t j", t=PACK),
+                dealt[:, :, first : first + count, :].rearrange("p t m j -> p m j t"),
+                raw.rearrange("p j (m t) -> p m j t", t=PACK),
             )
 
         def quantise(dealt, name, pieces, tag):
@@ -119,7 +119,6 @@ def tile_picked_zrandla_relu_po_kernel(
             )
 
         h_bf = keep.tile([P, S, PACK], BF16, name="h_bf", align_bytes=64)
-        h_codes = keep.tile([P, S], U32, name="h_codes", align_bytes=64)
         h_scales = keep.tile([P, S], U8, name="h_scales", align_bytes=64)
         h_banks = [bank(c, [P, PACK, CHUNK]) for c in range(CHUNKS)]
 
@@ -145,37 +144,37 @@ def tile_picked_zrandla_relu_po_kernel(
         w2_dealt = dealt_tile("w2_dealt", "w2_dealt")
         w2_codes = keep.tile([P, K_PASS], U32, name="w2_codes", tag="reused", align_bytes=64)
         w2_scales = keep.tile([P, K_PASS], U8, name="w2_scales", align_bytes=64)
-        w2_q = (w2_codes, w2_scales)
+        w2_q = (w2_codes, [w2_scales[:, t * P : (t + 1) * P] for t in range(PACK)])
 
-        def quantise_w2(t):
-            chans = slice(t * P, (t + 1) * P)
+        def quantise_w2(first, stop):
             nc.vector.quantize_mx(
-                out=w2_codes[:, chans].bitcast(FP8X4),
-                scales=w2_scales[:, chans],
-                in_=w2_dealt[:, t, :, :].rearrange("p m j -> p (m j)"),
+                out=w2_codes[:, first * P : stop * P].bitcast(FP8X4),
+                scales=w2_scales[:, first * P : stop * P],
+                in_=w2_dealt[:, first:stop, :, :].rearrange("p t m j -> p (t m j)"),
             )
 
+        for u, raw in enumerate(w2_raw):
+            deal(nc.vector.tensor_copy, w2_dealt, raw[:], u * N // 2)
+        h_codes = keep.tile([P, S], U32, name="h_codes", tag="w2_raw1", align_bytes=64)
+        quantise_w2(0, 1)
         for c in range(CHUNKS):
             cols = slice(c * CHUNK, (c + 1) * CHUNK)
-            if c < len(w2_raw):
-                deal(nc.vector.tensor_copy, w2_dealt, w2_raw[c][:], c * N // 2)
+            if c == CHUNKS - 1:
+                quantise_w2(1, 2)
             nc.scalar.activation(h_bf[:, cols, :], h_banks[c][:].rearrange("p t n -> p n t"), ACT.Relu)
             nc.vector.quantize_mx(
                 out=h_codes[:, cols].bitcast(FP8X4),
                 scales=h_scales[:, cols],
                 in_=h_bf[:, cols, :].rearrange("p n t -> p (n t)"),
             )
-            if c == len(w2_raw) - 1:
-                quantise_w2(0)
-        quantise_w2(1)
+        quantise_w2(2, PACK)
 
         def second_layer_pass(acc, w_q, t, cols):
-            codes, scales = w_q
-            chans = slice(t * P, (t + 1) * P)
+            codes, planes = w_q
             nc.tensor.matmul_mx(
                 out=acc,
-                lhsT=codes[:, chans].bitcast(FP8X4),
-                lhsT_scale=scales[:, chans],
+                lhsT=codes[:, t * P : (t + 1) * P].bitcast(FP8X4),
+                lhsT_scale=planes[t],
                 rhs=h_codes[:, cols].bitcast(FP8X4),
                 rhs_scale=h_scales[:, cols],
                 start=True,
@@ -203,48 +202,60 @@ def tile_picked_zrandla_relu_po_kernel(
         second_layer_pass(acc_1[:], w2_q, 1, slice(0, S))
         score = [keep.tile([P, S], F32, name="score%d" % t) for t in range(2)]
         nc.scalar.copy(score[0][:, most], acc_most[:])
-        nc.vector.tensor_copy(score[0][:, last], acc_last[:])
+        nc.scalar.copy(score[0][:, last], acc_last[:])
         nc.scalar.copy(score[1][:], acc_1[:])
-        for t in range(2, PACK):
-            quantise_w2(t)
         score.append(second_layer(w2_q, 2, "score2", 7))
         score.append(second_layer(w2_q, 3, "score3", 0))
         w3_dealt = dealt_tile("w3_dealt", "reused")
         deal(nc.scalar.copy, w3_dealt, w3_raw[:], 0)
 
-        s0, a = wide("s0"), wide("a")
-        q01 = keep.tile([P, 2, PACK, V], F32, name="q01", tag="w3_raw")
+        minus = keep.tile([P, V], F32, name="minus")
+        nc.gpsimd.memset(minus[:], -1.0)
+        q01 = keep.tile([P, 2, PACK, V], F32, name="q01", tag="w3_raw", align_bytes=64)
         q0, q1 = q01[:, 0, :, :], q01[:, 1, :, :]
         pairs = (slice(0, 2), slice(2, PACK))
-        every = slice(0, PACK)
 
-        def gather_first(t):
-            nc.vector.tensor_copy(s0[:, t, :], score[t][:].indirect(pos_sb[0][:]))
+        def gather_neg_s0(picked, t):
+            nc.vector.tensor_tensor(picked[:, 0, t % 2, :], score[t][:].indirect(pos_sb[0][:]), minus[:], ALU.mult)
 
-        def gather_difference(dst, t, d):
-            nc.vector.tensor_tensor(dst[:, t, :], score[t][:].indirect(pos_sb[d][:]), s0[:, t, :], ALU.subtract)
+        def gather_s2(picked, t):
+            nc.vector.tensor_copy(picked[:, 1, t % 2, :], score[t][:].indirect(pos_sb[2][:]))
 
-        gather_first(0)
-        for t in range(PACK):
-            if t + 1 < PACK:
-                gather_first(t + 1)
-            gather_difference(a, t, 1)
-        w3_q = quantise(w3_dealt, "w3", 1, "w3_codes")
-        b_relu = keep.tile([P, 2, PACK, V], F32, name="b_relu", tag="reused", align_bytes=64)
-        b, neg_relu = b_relu[:, 0, :, :], b_relu[:, 1, :, :]
-        for t in range(PACK):
-            gather_difference(b, t, 2)
-        nc.vector.tensor_scalar(flat(neg_relu, every), flat(a, every), -1.0, 0.0, ALU.mult, ALU.min)
-        for ts in pairs:
-            nc.scalar.activation(flat(q1, ts), flat(a, ts), ACT.Sigmoid)
-            nc.scalar.activation(flat(q0, ts), flat(a, ts), ACT.Sigmoid, scale=-1.0)
+        def gather_a(picked, t):
+            nc.vector.tensor_tensor(
+                picked[:, 2, t % 2, :], score[t][:].indirect(pos_sb[1][:]), picked[:, 0, t % 2, :], ALU.add
+            )
 
-        mag, log_q = wide("mag"), wide("log_q")
-        nc.scalar.activation(flat(mag, every), flat(q1, every), ACT.Abs, bias=-0.5)
-        feat = [second_layer(w3_q, t, "feat%d" % t, 1 + t) for t in range(2)]
-        for ts in pairs:
-            nc.scalar.activation(flat(log_q, ts), flat(mag, ts), ACT.Ln, bias=0.5)
-        feat.extend(second_layer(w3_q, t, "feat%d" % t, 1 + t) for t in range(2, PACK))
+        picked = [keep.tile([P, 3, 2, V], F32, name="picked0")]
+        for t in range(2):
+            for gather in (gather_neg_s0, gather_s2, gather_a):
+                gather(picked[0], t)
+        w3_codes, w3_scales = quantise(w3_dealt, "w3", 1, "w3_codes")
+        w3_q = (w3_codes, [w3_scales[:, t * P : (t + 1) * P] for t in range(PACK)])
+        picked.append(keep.tile([P, 3, 2, V], F32, name="picked1", tag="reused", align_bytes=64))
+        for gather in (gather_neg_s0, gather_a, gather_s2):
+            for t in range(2, PACK):
+                gather(picked[1], t)
+        neg_s0, s2, a = (
+            [tile[:, n, :, :].rearrange("p t v -> p (t v)") for tile in picked] for n in range(3)
+        )
+
+        def pair_weights(u):
+            nc.scalar.activation(flat(q1, pairs[u]), a[u], ACT.Sigmoid)
+            nc.scalar.activation(flat(q0, pairs[u]), a[u], ACT.Sigmoid, scale=-1.0)
+
+        pair_weights(0)
+        feat = [second_layer(w3_q, t, "feat%d" % t, 1 + t) for t in range(PACK)]
+        pair_weights(1)
+        neg_relu = wide("neg_relu")
+        for u in (1, 0):
+            nc.vector.tensor_scalar(flat(neg_relu, pairs[u]), a[u], -1.0, 0.0, ALU.mult, ALU.min)
+        log_q = wide("log_q")
+        mag = [keep.tile([P, 2 * V], F32, name="mag%d" % u) for u in range(2)]
+        for u, ts in enumerate(pairs):
+            nc.scalar.activation(mag[u][:], flat(q1, ts), ACT.Abs, bias=-0.5)
+        for u, ts in enumerate(pairs):
+            nc.scalar.activation(flat(log_q, ts), mag[u][:], ACT.Ln, bias=0.5)
 
         def add_turned(acc, terms):
             blocks = acc.shape[1]
@@ -263,36 +274,39 @@ def tile_picked_zrandla_relu_po_kernel(
         keep01 = []
         for u, ts in enumerate(pairs):
             c_turned = bank(5 + u, [P, 2 * halves, P])
-            add_turned(c_turned, [flat(term, ts) for term in (b, neg_relu, log_q)])
+            add_turned(c_turned, (neg_s0[u], s2[u], flat(neg_relu, ts), flat(log_q, ts)))
             weight = keep.tile([P, 2 * halves, P], F32, name="keep01_%d" % u)
             nc.scalar.activation(weight[:], c_turned[:], ACT.Sigmoid, scale=-1.0)
             keep01.append(weight)
 
-        minus = keep.tile([P, V], F32, name="minus")
-        nc.gpsimd.memset(minus[:], -1.0)
-        neg_y2, z1, res = (wide(name) for name in ("neg_y2", "z1", "res"))
-        z0 = [keep.tile([P, 2, V], F32, name=name) for name in ("z0", "log_q")]
-        diff = []
-        for t in range(PACK):
-            terms = (z0[t // 2][:, t % 2, :], neg_y2[:, t, :], z1[:, t, :])
-            for dst, d, factor in zip(terms, (0, 2, 1), (q0[:, t, :], minus[:], q1[:, t, :])):
-                nc.vector.tensor_tensor(dst, feat[t][:].indirect(pos_sb[d][:]), factor, ALU.mult)
-            acc = bank((7 + t) % 8, [P, halves, P])
-            add_turned(acc, terms)
+        res = wide("res")
+
+        def gather_feature(dst, t, d, factor):
+            nc.vector.tensor_tensor(dst, feat[t][:].indirect(pos_sb[d][:]), factor, ALU.mult)
+
+        diff, neg_y2 = [], []
+        for u, ts in enumerate(pairs):
+            z = keep.tile([P, 3, 2, V], F32, name=("z", "mag0")[u])
+            for d in (2, 0, 1):
+                for t in range(ts.start, ts.stop):
+                    gather_feature(z[:, d, t % 2, :], t, d, (q0[:, t, :], q1[:, t, :], minus[:])[d])
+            neg_y2.extend(z[:, 2, n, :] for n in range(2))
+            acc = bank((7, 4)[u], [P, 2 * halves, P])
+            add_turned(acc, [flat(z[:, d, :, :], slice(0, 2)) for d in (2, 0, 1)])
             diff.append(acc)
 
         back = []
         for t in range(PACK):
             step = keep.tile([P, halves, P], F32, name="step%d" % t)
-            first = (t % 2) * halves
-            nc.vector.tensor_tensor(step[:], diff[t][:], keep01[t // 2][:, first : first + halves, :], ALU.mult)
-            acc = bank(3 + t, [P, V])
+            blocks = slice((t % 2) * halves, (t % 2 + 1) * halves)
+            nc.vector.tensor_tensor(step[:], diff[t // 2][:, blocks, :], keep01[t // 2][:, blocks, :], ALU.mult)
+            acc = bank(t, [P, V])
             for i in range(halves):
                 nc.tensor.transpose(acc[:, i * P : (i + 1) * P], step[:, i, :], ident[:])
             back.append(acc)
         out_rows = out_0.rearrange("(p t) v -> p t v", t=PACK)
         for t in range(PACK):
-            nc.vector.tensor_tensor(res[:, t, :], back[t][:], neg_y2[:, t, :], ALU.subtract)
+            nc.vector.tensor_tensor(res[:, t, :], back[t][:], neg_y2[t], ALU.subtract)
             if t % 2:
                 nc.sync.dma_start(out=out_rows[:, pairs[t // 2], :], in_=res[:, pairs[t // 2], :])
 
@@ -300,8 +314,11 @@ def tile_picked_zrandla_relu_po_kernel(
         o_scales = keep.tile([P, V], U8, name="o_scales", align_bytes=64)
         centres = [slice(0, V // 2), slice(V // 2, V)]
         res_bf = [keep.tile([P, V // 2, PACK], BF16, name="res_bf%d" % i, align_bytes=64) for i in range(2)]
-        nc.scalar.copy(res_bf[1][:], res[:, :, centres[1]].rearrange("p t v -> p v t"))
-        nc.vector.tensor_copy(res_bf[0][:], res[:, :, centres[0]].rearrange("p t v -> p v t"))
+        for copy, i in ((nc.scalar.copy, 1), (nc.vector.tensor_copy, 0)):
+            copy(
+                res_bf[i][:].rearrange("p (c n) t -> p c t n", n=PACK),
+                res[:, :, centres[i]].rearrange("p t (c n) -> p c t n", n=PACK),
+            )
         for i, vs in enumerate(centres):
             nc.vector.quantize_mx(
                 out=o_codes[:, vs].bitcast(FP8X4),

@@ -26,6 +26,7 @@ SCALE_ROWS = 4
 LIST_ROWS = 16
 CHUNK = 128
 CHUNKS = S // CHUNK
+CLAMP = 24.0
 W1_SCALAR_COLS = 192
 
 
@@ -93,7 +94,7 @@ def tile_picked_zrandla_relu_po_kernel(
             xw_table.append(table)
         w2_raw = [load_weight(w2[:, u * N // 2 : (u + 1) * N // 2], "w2_raw%d" % u) for u in range(2)]
         pos_sb = [load_list(src, "pos%d_sb" % d) for d, src in enumerate((pos1, pos2, pos3))]
-        w3_raw = load_weight(w3, "w3_raw")
+        w3_raw = [load_weight(w3[:, u * N // 2 : (u + 1) * N // 2], "w3_raw%d" % u) for u in range(2)]
 
         ident = keep.tile([P, P], F32, name="ident")
         make_identity(nc, ident[:])
@@ -143,7 +144,7 @@ def tile_picked_zrandla_relu_po_kernel(
 
         w2_dealt = dealt_tile("w2_dealt", "w2_dealt")
         w2_codes = keep.tile([P, K_PASS], U32, name="w2_codes", tag="reused", align_bytes=64)
-        w2_scales = keep.tile([P, K_PASS], U8, name="w2_scales", align_bytes=64)
+        w2_scales = keep.tile([P, K_PASS], U8, name="w2_scales", tag="w2_scales", align_bytes=64)
         w2_q = (w2_codes, [w2_scales[:, t * P : (t + 1) * P] for t in range(PACK)])
 
         def quantise_w2(first, stop):
@@ -159,15 +160,18 @@ def tile_picked_zrandla_relu_po_kernel(
         quantise_w2(0, 1)
         for c in range(CHUNKS):
             cols = slice(c * CHUNK, (c + 1) * CHUNK)
-            if c == CHUNKS - 1:
+            if c == CHUNKS - 2:
                 quantise_w2(1, 2)
+            if c == CHUNKS - 1:
+                quantise_w2(2, PACK)
             nc.scalar.activation(h_bf[:, cols, :], h_banks[c][:].rearrange("p t n -> p n t"), ACT.Relu)
             nc.vector.quantize_mx(
                 out=h_codes[:, cols].bitcast(FP8X4),
                 scales=h_scales[:, cols],
                 in_=h_bf[:, cols, :].rearrange("p n t -> p (n t)"),
             )
-        quantise_w2(2, PACK)
+        w3_dealt = dealt_tile("w3_dealt", "w3_dealt")
+        deal(nc.vector.tensor_copy, w3_dealt, w3_raw[0][:], 0)
 
         def second_layer_pass(acc, w_q, t, cols):
             codes, planes = w_q
@@ -191,9 +195,6 @@ def tile_picked_zrandla_relu_po_kernel(
         def wide(name):
             return keep.tile([P, PACK, V], F32, name=name)
 
-        def flat(tile, ts):
-            return tile[:, ts, :].rearrange("p t v -> p (t v)")
-
         most, last = slice(0, S - CHUNK), slice(S - CHUNK, S)
         acc_most, acc_last, acc_1 = bank(4, [P, S - CHUNK]), bank(5, [P, CHUNK]), bank(6, [P, S])
         for cols in (slice(0, 2 * CHUNK), slice(2 * CHUNK, 3 * CHUNK)):
@@ -205,94 +206,110 @@ def tile_picked_zrandla_relu_po_kernel(
         nc.scalar.copy(score[0][:, last], acc_last[:])
         nc.scalar.copy(score[1][:], acc_1[:])
         score.append(second_layer(w2_q, 2, "score2", 7))
-        score.append(second_layer(w2_q, 3, "score3", 0))
-        w3_dealt = dealt_tile("w3_dealt", "reused")
-        deal(nc.scalar.copy, w3_dealt, w3_raw[:], 0)
+        score.append(second_layer(w2_q, 3, "score3", 6))
+        deal(nc.scalar.copy, w3_dealt, w3_raw[1][:], N // 2)
+
+        pairs = (slice(0, 2), slice(2, PACK))
+
+        def pair_tile(name, tag=None):
+            return keep.tile([P, 2, V], F32, name=name, tag=tag or name, align_bytes=64)
+
+        def both(tile):
+            return tile[:, :, :].rearrange("p t v -> p (t v)")
 
         minus = keep.tile([P, V], F32, name="minus")
         nc.gpsimd.memset(minus[:], -1.0)
-        q01 = keep.tile([P, 2, PACK, V], F32, name="q01", tag="w3_raw", align_bytes=64)
-        q0, q1 = q01[:, 0, :, :], q01[:, 1, :, :]
-        pairs = (slice(0, 2), slice(2, PACK))
 
-        def gather_neg_s0(picked, t):
-            nc.vector.tensor_tensor(picked[:, 0, t % 2, :], score[t][:].indirect(pos_sb[0][:]), minus[:], ALU.mult)
+        def gather(dst, rows, d, other, op):
+            nc.vector.tensor_tensor(dst, rows[:].indirect(pos_sb[d][:]), other, op)
 
-        def gather_s2(picked, t):
-            nc.vector.tensor_copy(picked[:, 1, t % 2, :], score[t][:].indirect(pos_sb[2][:]))
-
-        def gather_a(picked, t):
-            nc.vector.tensor_tensor(
-                picked[:, 2, t % 2, :], score[t][:].indirect(pos_sb[1][:]), picked[:, 0, t % 2, :], ALU.add
-            )
-
-        picked = [keep.tile([P, 3, 2, V], F32, name="picked0")]
-        for t in range(2):
-            for gather in (gather_neg_s0, gather_s2, gather_a):
-                gather(picked[0], t)
-        w3_codes, w3_scales = quantise(w3_dealt, "w3", 1, "w3_codes")
+        after_w3 = keep.tile([P, 2, 2, V], F32, name="after_w3", tag="w3_raw1", align_bytes=64)
+        neg_s1, u01 = [], []
+        for n, ts in enumerate(pairs):
+            neg_s1.append(pair_tile("neg_s1_%d" % n, None if n else "w3_raw0"))
+            for t in range(ts.start, ts.stop):
+                gather(neg_s1[n][:, t % 2, :], score[t], 1, minus[:], ALU.mult)
+            if n:
+                w3_codes, w3_scales = quantise(w3_dealt, "w3", 1, "w3_codes")
+            u01.append(after_w3[:, 0, :, :] if n else pair_tile("u0", "w2_scales"))
+            for t in range(ts.start, ts.stop):
+                gather(u01[n][:, t % 2, :], score[t], 0, neg_s1[n][:, t % 2, :], ALU.add)
         w3_q = (w3_codes, [w3_scales[:, t * P : (t + 1) * P] for t in range(PACK)])
-        picked.append(keep.tile([P, 3, 2, V], F32, name="picked1", tag="reused", align_bytes=64))
-        for gather in (gather_neg_s0, gather_a, gather_s2):
-            for t in range(2, PACK):
-                gather(picked[1], t)
-        neg_s0, s2, a = (
-            [tile[:, n, :, :].rearrange("p t v -> p (t v)") for tile in picked] for n in range(3)
-        )
 
-        def pair_weights(u):
-            nc.scalar.activation(flat(q1, pairs[u]), a[u], ACT.Sigmoid)
-            nc.scalar.activation(flat(q0, pairs[u]), a[u], ACT.Sigmoid, scale=-1.0)
+        rho = [after_w3[:, 1, :, :], pair_tile("rho1")]
+        rest = []
+        q0 = [pair_tile("q0_%d" % n) for n in range(2)]
+        q1 = [pair_tile("q1_%d" % n) for n in range(2)]
 
-        pair_weights(0)
-        feat = [second_layer(w3_q, t, "feat%d" % t, 1 + t) for t in range(PACK)]
-        pair_weights(1)
-        neg_relu = wide("neg_relu")
-        for u in (1, 0):
-            nc.vector.tensor_scalar(flat(neg_relu, pairs[u]), a[u], -1.0, 0.0, ALU.mult, ALU.min)
-        log_q = wide("log_q")
-        mag = [keep.tile([P, 2 * V], F32, name="mag%d" % u) for u in range(2)]
-        for u, ts in enumerate(pairs):
-            nc.scalar.activation(mag[u][:], flat(q1, ts), ACT.Abs, bias=-0.5)
-        for u, ts in enumerate(pairs):
-            nc.scalar.activation(flat(log_q, ts), mag[u][:], ACT.Ln, bias=0.5)
+        def clamp(n):
+            nc.scalar.activation(both(rho[n]), both(u01[n]), ACT.Relu, bias=CLAMP)
+            rest.append(pair_tile("rest%d" % n))
+            for t in range(pairs[n].start, pairs[n].stop):
+                gather(rest[n][:, t % 2, :], score[t], 2, rho[n][:, t % 2, :], ALU.subtract)
 
-        def add_turned(acc, terms):
-            blocks = acc.shape[1]
-            for n, term in enumerate(terms):
-                for i in range(blocks):
+        def first_weight(n):
+            nc.scalar.activation(both(q0[n]), both(rho[n]), ACT.Sigmoid, bias=-CLAMP)
+
+        def second_weight(dst, src):
+            nc.scalar.activation(dst, src, ACT.Sigmoid, scale=-1.0, bias=CLAMP)
+
+        def features(t):
+            feat.append(second_layer(w3_q, t, "feat%d" % t, 1 + t))
+
+        feat = []
+        clamp(0)
+        first_weight(0)
+        second_weight(both(q1[0]), both(rho[0]))
+        features(0)
+        clamp(1)
+        features(1)
+        first_weight(1)
+        second_weight(q1[1][:, 0, :], rho[1][:, 0, :])
+        features(2)
+        log_q = [pair_tile("log_q%d" % n) for n in range(2)]
+        for n in range(2):
+            nc.scalar.activation(both(log_q[n]), both(q0[n]), ACT.Ln)
+        features(3)
+        second_weight(q1[1][:, 1, :], rho[1][:, 1, :])
+
+        def add_turned(acc, terms, opens, closes):
+            for n, (t, rows) in enumerate(terms):
+                for i in range(halves):
                     nc.tensor.matmul(
-                        acc[:, i, :],
-                        term[:, i * P : (i + 1) * P],
+                        acc[:, (t % 2) * halves + i, :],
+                        rows[:, i * P : (i + 1) * P],
                         ident[:],
-                        start=(n == 0 and i == 0),
-                        stop=(n == len(terms) - 1 and i == blocks - 1),
+                        start=(opens and n == 0 and i == 0),
+                        stop=(closes and n == len(terms) - 1 and i == halves - 1),
                         is_transpose=True,
                     )
 
+        def by_t(tile):
+            return [(t, tile[:, t, :]) for t in range(2)]
+
         halves = V // P
         keep01 = []
-        for u, ts in enumerate(pairs):
-            c_turned = bank(5 + u, [P, 2 * halves, P])
-            add_turned(c_turned, (neg_s0[u], s2[u], flat(neg_relu, ts), flat(log_q, ts)))
-            weight = keep.tile([P, 2 * halves, P], F32, name="keep01_%d" % u)
-            nc.scalar.activation(weight[:], c_turned[:], ACT.Sigmoid, scale=-1.0)
+        for n in range(2):
+            c_turned = bank(5 + n, [P, 2 * halves, P])
+            add_turned(c_turned, by_t(neg_s1[n]) + by_t(rest[n]) + by_t(log_q[n]), True, True)
+            weight = keep.tile([P, 2 * halves, P], F32, name="keep01_%d" % n)
+            nc.scalar.activation(weight[:], c_turned[:], ACT.Sigmoid, scale=-1.0, bias=-CLAMP)
             keep01.append(weight)
 
         res = wide("res")
-
-        def gather_feature(dst, t, d, factor):
-            nc.vector.tensor_tensor(dst, feat[t][:].indirect(pos_sb[d][:]), factor, ALU.mult)
-
         diff, neg_y2 = [], []
-        for u, ts in enumerate(pairs):
-            z = keep.tile([P, 3, 2, V], F32, name=("z", "mag0")[u])
-            for d in (2, 0, 1):
+        for n, ts in enumerate(pairs):
+            last = pair_tile("neg_y2_%d" % n)
+            z = keep.tile([P, 2, 2, V], F32, name="z%d" % n, tag=("z0", "q0_0")[n], align_bytes=64)
+            for t in range(ts.start, ts.stop):
+                gather(last[:, t % 2, :], feat[t], 2, minus[:], ALU.mult)
+            for d, q in enumerate((q0[n], q1[n])):
                 for t in range(ts.start, ts.stop):
-                    gather_feature(z[:, d, t % 2, :], t, d, (q0[:, t, :], q1[:, t, :], minus[:])[d])
-            neg_y2.extend(z[:, 2, n, :] for n in range(2))
-            acc = bank((7, 4)[u], [P, 2 * halves, P])
-            add_turned(acc, [flat(z[:, d, :, :], slice(0, 2)) for d in (2, 0, 1)])
+                    gather(z[:, d, t % 2, :], feat[t], d, q[:, t % 2, :], ALU.mult)
+            neg_y2.extend(last[:, t, :] for t in range(2))
+            first, second = by_t(z[:, 0, :, :]), by_t(z[:, 1, :, :])
+            acc = bank((7, 4)[n], [P, 2 * halves, P])
+            add_turned(acc, first[0:1] + by_t(last) + first[1:2] + second, True, True)
             diff.append(acc)
 
         back = []

@@ -26,6 +26,7 @@ SCALE_ROWS = 4
 LIST_ROWS = 16
 CHUNK = 128
 CHUNKS = S // CHUNK
+HUGE = 2.0**127
 CLAMP = 24.0
 W1_SCALAR_COLS = 192
 
@@ -160,18 +161,26 @@ def tile_picked_zrandla_relu_po_kernel(
         quantise_w2(0, 1)
         for c in range(CHUNKS):
             cols = slice(c * CHUNK, (c + 1) * CHUNK)
-            if c == CHUNKS - 2:
-                quantise_w2(1, 2)
             if c == CHUNKS - 1:
-                quantise_w2(2, PACK)
+                quantise_w2(1, 2)
             nc.scalar.activation(h_bf[:, cols, :], h_banks[c][:].rearrange("p t n -> p n t"), ACT.Relu)
             nc.vector.quantize_mx(
                 out=h_codes[:, cols].bitcast(FP8X4),
                 scales=h_scales[:, cols],
                 in_=h_bf[:, cols, :].rearrange("p n t -> p (n t)"),
             )
-        w3_dealt = dealt_tile("w3_dealt", "w3_dealt")
-        deal(nc.vector.tensor_copy, w3_dealt, w3_raw[0][:], 0)
+        quantise_w2(2, PACK)
+
+        w3_dealt = dealt_tile("w3_dealt", "w2_dealt")
+        for first in range(0, N // 2, P):
+            nc.gpsimd.tensor_scalar(
+                w3_dealt[:, :, first // PACK : (first + P) // PACK, :],
+                w3_raw[0][:, :, first : first + P].rearrange("p j (m t) -> p t m j", t=PACK),
+                1.0,
+                0.0,
+                ALU.mult,
+                ALU.add,
+            )
 
         def second_layer_pass(acc, w_q, t, cols):
             codes, planes = w_q
@@ -185,11 +194,11 @@ def tile_picked_zrandla_relu_po_kernel(
                 stop=True,
             )
 
-        def second_layer(w_q, t, name, index):
+        def second_layer(w_q, t, name, index, sign):
             acc = bank(index, [P, S])
             second_layer_pass(acc[:], w_q, t, slice(0, S))
             row = keep.tile([P, S], F32, name=name)
-            nc.scalar.copy(row[:], acc[:])
+            nc.scalar.mul(row[:], acc[:], sign)
             return row
 
         def wide(name):
@@ -202,11 +211,11 @@ def tile_picked_zrandla_relu_po_kernel(
         second_layer_pass(acc_last[:], w2_q, 0, last)
         second_layer_pass(acc_1[:], w2_q, 1, slice(0, S))
         score = [keep.tile([P, S], F32, name="score%d" % t) for t in range(2)]
-        nc.scalar.copy(score[0][:, most], acc_most[:])
-        nc.scalar.copy(score[0][:, last], acc_last[:])
-        nc.scalar.copy(score[1][:], acc_1[:])
-        score.append(second_layer(w2_q, 2, "score2", 7))
-        score.append(second_layer(w2_q, 3, "score3", 6))
+        nc.scalar.mul(score[0][:, most], acc_most[:], -1.0)
+        nc.scalar.mul(score[0][:, last], acc_last[:], -1.0)
+        nc.scalar.mul(score[1][:], acc_1[:], -1.0)
+        score.append(second_layer(w2_q, 2, "score2", 7, -1.0))
+        score.append(second_layer(w2_q, 3, "score3", 6, -1.0))
         deal(nc.scalar.copy, w3_dealt, w3_raw[1][:], N // 2)
 
         pairs = (slice(0, 2), slice(2, PACK))
@@ -223,55 +232,52 @@ def tile_picked_zrandla_relu_po_kernel(
         def gather(dst, rows, d, other, op):
             nc.vector.tensor_tensor(dst, rows[:].indirect(pos_sb[d][:]), other, op)
 
-        after_w3 = keep.tile([P, 2, 2, V], F32, name="after_w3", tag="w3_raw1", align_bytes=64)
-        neg_s1, u01 = [], []
-        for n, ts in enumerate(pairs):
-            neg_s1.append(pair_tile("neg_s1_%d" % n, None if n else "w3_raw0"))
-            for t in range(ts.start, ts.stop):
-                gather(neg_s1[n][:, t % 2, :], score[t], 1, minus[:], ALU.mult)
-            if n:
-                w3_codes, w3_scales = quantise(w3_dealt, "w3", 1, "w3_codes")
-            u01.append(after_w3[:, 0, :, :] if n else pair_tile("u0", "w2_scales"))
-            for t in range(ts.start, ts.stop):
-                gather(u01[n][:, t % 2, :], score[t], 0, neg_s1[n][:, t % 2, :], ALU.add)
-        w3_q = (w3_codes, [w3_scales[:, t * P : (t + 1) * P] for t in range(PACK)])
+        def gather_neg_s1(n):
+            for t in range(2):
+                nc.vector.tensor_copy(neg_s1[n][:, t, :], score[2 * n + t][:].indirect(pos_sb[1][:]))
 
-        rho = [after_w3[:, 1, :, :], pair_tile("rho1")]
-        rest = []
+        def gather_a(n):
+            for t in range(2):
+                gather(a[n][:, t, :], score[2 * n + t], 0, neg_s1[n][:, t, :], ALU.subtract)
+
+        second = keep.tile([P, 2, 2, V], F32, name="second", tag="w2_scales", align_bytes=64)
+        neg_s1 = [pair_tile("neg_s1_0"), second[:, 1, :, :]]
+        cut = [pair_tile("cut%d" % n) for n in range(2)]
+        a = [second[:, 0, :, :]]
+        gather_neg_s1(0)
+        gather_a(0)
+        nc.gpsimd.tensor_scalar(both(cut[0]), both(a[0]), CLAMP, -HUGE, ALU.min, ALU.max)
+        gather_neg_s1(1)
+        w3_codes, w3_scales = quantise(w3_dealt, "w3", 1, "w3_codes")
+        w3_q = (w3_codes, [w3_scales[:, t * P : (t + 1) * P] for t in range(PACK)])
+        third = keep.tile([P, 3, 2, V], F32, name="third", tag="w3_raw1", align_bytes=64)
+        a.append(third[:, 0, :, :])
+        s2 = [third[:, 1 + n, :, :] for n in range(2)]
+        gather_a(1)
+        for t in range(PACK):
+            gather(s2[t // 2][:, t % 2, :], score[t], 2, minus[:], ALU.mult)
+            if t == 0:
+                nc.vector.tensor_scalar_min(both(cut[1]), both(a[1]), CLAMP)
         q0 = [pair_tile("q0_%d" % n) for n in range(2)]
         q1 = [pair_tile("q1_%d" % n) for n in range(2)]
 
-        def clamp(n):
-            nc.scalar.activation(both(rho[n]), both(u01[n]), ACT.Relu, bias=CLAMP)
-            rest.append(pair_tile("rest%d" % n))
-            for t in range(pairs[n].start, pairs[n].stop):
-                gather(rest[n][:, t % 2, :], score[t], 2, rho[n][:, t % 2, :], ALU.subtract)
-
         def first_weight(n):
-            nc.scalar.activation(both(q0[n]), both(rho[n]), ACT.Sigmoid, bias=-CLAMP)
+            nc.scalar.activation(both(q0[n]), both(cut[n]), ACT.Sigmoid, scale=-1.0)
 
         def second_weight(dst, src):
-            nc.scalar.activation(dst, src, ACT.Sigmoid, scale=-1.0, bias=CLAMP)
+            nc.scalar.activation(dst, src, ACT.Sigmoid)
 
         def features(t):
-            feat.append(second_layer(w3_q, t, "feat%d" % t, 1 + t))
+            feat.append(second_layer(w3_q, t, "feat%d" % t, 1 + t, 1.0))
 
         feat = []
-        clamp(0)
         first_weight(0)
-        second_weight(both(q1[0]), both(rho[0]))
-        features(0)
-        clamp(1)
-        features(1)
+        second_weight(both(q1[0]), both(cut[0]))
+        for t in range(PACK - 1):
+            features(t)
         first_weight(1)
-        second_weight(q1[1][:, 0, :], rho[1][:, 0, :])
-        features(2)
-        log_q = [pair_tile("log_q%d" % n) for n in range(2)]
-        for n in range(2):
-            nc.scalar.activation(both(log_q[n]), both(q0[n]), ACT.Ln)
-        features(3)
-        second_weight(q1[1][:, 1, :], rho[1][:, 1, :])
-
+        second_weight(q1[1][:, 0, :], cut[1][:, 0, :])
+        features(PACK - 1)
         def add_turned(acc, terms, opens, closes):
             for n, (t, rows) in enumerate(terms):
                 for i in range(halves):
@@ -288,12 +294,20 @@ def tile_picked_zrandla_relu_po_kernel(
             return [(t, tile[:, t, :]) for t in range(2)]
 
         halves = V // P
+        c_turned = [bank(6 + n, [P, 2 * halves, P]) for n in range(2)]
+        for n in range(2):
+            add_turned(c_turned[n], by_t(neg_s1[n]) + by_t(cut[n]) + by_t(s2[n]), True, False)
+        log_both = keep.tile([P, 2, 2, V], F32, name="log_q", tag="w3_raw1", align_bytes=64)
+        log_q = [log_both[:, n, :, :] for n in range(2)]
+        for n in range(2):
+            nc.scalar.activation(both(log_q[n]), both(q0[n]), ACT.Ln)
+        second_weight(q1[1][:, 1, :], cut[1][:, 1, :])
+
         keep01 = []
         for n in range(2):
-            c_turned = bank(5 + n, [P, 2 * halves, P])
-            add_turned(c_turned, by_t(neg_s1[n]) + by_t(rest[n]) + by_t(log_q[n]), True, True)
+            add_turned(c_turned[n], by_t(log_q[n]), False, True)
             weight = keep.tile([P, 2 * halves, P], F32, name="keep01_%d" % n)
-            nc.scalar.activation(weight[:], c_turned[:], ACT.Sigmoid, scale=-1.0, bias=-CLAMP)
+            nc.scalar.activation(weight[:], c_turned[n][:], ACT.Sigmoid, scale=-1.0)
             keep01.append(weight)
 
         res = wide("res")
@@ -308,7 +322,7 @@ def tile_picked_zrandla_relu_po_kernel(
                     gather(z[:, d, t % 2, :], feat[t], d, q[:, t % 2, :], ALU.mult)
             neg_y2.extend(last[:, t, :] for t in range(2))
             first, second = by_t(z[:, 0, :, :]), by_t(z[:, 1, :, :])
-            acc = bank((7, 4)[n], [P, 2 * halves, P])
+            acc = bank((5, 4)[n], [P, 2 * halves, P])
             add_turned(acc, first[0:1] + by_t(last) + first[1:2] + second, True, True)
             diff.append(acc)
 

@@ -95,7 +95,7 @@ def tile_picked_zrandla_relu_po_kernel(
             xw_table.append(table)
         w2_raw = [load_weight(w2[:, u * N // 2 : (u + 1) * N // 2], "w2_raw%d" % u) for u in range(2)]
         pos_sb = [load_list(src, "pos%d_sb" % d) for d, src in enumerate((pos1, pos2, pos3))]
-        w3_raw = [load_weight(w3[:, u * N // 2 : (u + 1) * N // 2], "w3_raw%d" % u) for u in range(2)]
+        w3_raw = load_weight(w3, "w3_raw")
 
         ident = keep.tile([P, P], F32, name="ident")
         make_identity(nc, ident[:])
@@ -171,16 +171,6 @@ def tile_picked_zrandla_relu_po_kernel(
             )
         quantise_w2(2, PACK)
 
-        w3_dealt = dealt_tile("w3_dealt", "w2_dealt")
-        for first in range(0, N // 2, P):
-            nc.gpsimd.tensor_scalar(
-                w3_dealt[:, :, first // PACK : (first + P) // PACK, :],
-                w3_raw[0][:, :, first : first + P].rearrange("p j (m t) -> p t m j", t=PACK),
-                1.0,
-                0.0,
-                ALU.mult,
-                ALU.add,
-            )
 
         def second_layer_pass(acc, w_q, t, cols):
             codes, planes = w_q
@@ -216,7 +206,8 @@ def tile_picked_zrandla_relu_po_kernel(
         nc.scalar.mul(score[1][:], acc_1[:], -1.0)
         score.append(second_layer(w2_q, 2, "score2", 7, -1.0))
         score.append(second_layer(w2_q, 3, "score3", 6, -1.0))
-        deal(nc.scalar.copy, w3_dealt, w3_raw[1][:], N // 2)
+        w3_dealt = dealt_tile("w3_dealt", "reused")
+        deal(nc.scalar.copy, w3_dealt, w3_raw[:], 0)
 
         pairs = (slice(0, 2), slice(2, PACK))
 
@@ -242,22 +233,22 @@ def tile_picked_zrandla_relu_po_kernel(
 
         second = keep.tile([P, 2, 2, V], F32, name="second", tag="w2_scales", align_bytes=64)
         neg_s1 = [pair_tile("neg_s1_0"), second[:, 1, :, :]]
-        cut = [pair_tile("cut%d" % n) for n in range(2)]
+        cut = [pair_tile("cut0")]
         a = [second[:, 0, :, :]]
         gather_neg_s1(0)
         gather_a(0)
         nc.gpsimd.tensor_scalar(both(cut[0]), both(a[0]), CLAMP, -HUGE, ALU.min, ALU.max)
         gather_neg_s1(1)
+        a.append(pair_tile("a1", "log_q"))
+        gather_a(1)
         w3_codes, w3_scales = quantise(w3_dealt, "w3", 1, "w3_codes")
         w3_q = (w3_codes, [w3_scales[:, t * P : (t + 1) * P] for t in range(PACK)])
-        third = keep.tile([P, 3, 2, V], F32, name="third", tag="w3_raw1", align_bytes=64)
-        a.append(third[:, 0, :, :])
+        third = keep.tile([P, 3, 2, V], F32, name="third", tag="w3_raw", align_bytes=64)
+        cut.append(third[:, 0, :, :])
         s2 = [third[:, 1 + n, :, :] for n in range(2)]
-        gather_a(1)
+        nc.vector.tensor_scalar_min(both(cut[1]), both(a[1]), CLAMP)
         for t in range(PACK):
             gather(s2[t // 2][:, t % 2, :], score[t], 2, minus[:], ALU.mult)
-            if t == 0:
-                nc.vector.tensor_scalar_min(both(cut[1]), both(a[1]), CLAMP)
         q0 = [pair_tile("q0_%d" % n) for n in range(2)]
         q1 = [pair_tile("q1_%d" % n) for n in range(2)]
 
@@ -273,9 +264,10 @@ def tile_picked_zrandla_relu_po_kernel(
         feat = []
         first_weight(0)
         second_weight(both(q1[0]), both(cut[0]))
-        for t in range(PACK - 1):
-            features(t)
+        features(0)
+        features(1)
         first_weight(1)
+        features(2)
         second_weight(q1[1][:, 0, :], cut[1][:, 0, :])
         features(PACK - 1)
         def add_turned(acc, terms, opens, closes):
@@ -297,7 +289,7 @@ def tile_picked_zrandla_relu_po_kernel(
         c_turned = [bank(6 + n, [P, 2 * halves, P]) for n in range(2)]
         for n in range(2):
             add_turned(c_turned[n], by_t(neg_s1[n]) + by_t(cut[n]) + by_t(s2[n]), True, False)
-        log_both = keep.tile([P, 2, 2, V], F32, name="log_q", tag="w3_raw1", align_bytes=64)
+        log_both = keep.tile([P, 2, 2, V], F32, name="log_q", tag="log_q", align_bytes=64)
         log_q = [log_both[:, n, :, :] for n in range(2)]
         for n in range(2):
             nc.scalar.activation(both(log_q[n]), both(q0[n]), ACT.Ln)

@@ -312,41 +312,49 @@ def tile_picked_zrandla_relu_po_kernel(
             for d, q in enumerate((q0[n], q1[n])):
                 for t in range(ts.start, ts.stop):
                     gather(z[:, d, t % 2, :], feat[t], d, q[:, t % 2, :], ALU.mult)
-            neg_y2.extend(last[:, t, :] for t in range(2))
+            neg_y2.append(last)
             first, second = by_t(z[:, 0, :, :]), by_t(z[:, 1, :, :])
             acc = bank((5, 4)[n], [P, 2 * halves, P])
             add_turned(acc, first[0:1] + by_t(last) + first[1:2] + second, True, True)
             diff.append(acc)
 
+        centres = [slice(0, V // 2), slice(V // 2, V)]
         back = []
-        for t in range(PACK):
-            step = keep.tile([P, halves, P], F32, name="step%d" % t)
-            blocks = slice((t % 2) * halves, (t % 2 + 1) * halves)
-            nc.vector.tensor_tensor(step[:], diff[t // 2][:, blocks, :], keep01[t // 2][:, blocks, :], ALU.mult)
-            acc = bank(t, [P, V])
+        for piece in range(PACK):
+            step = keep.tile([P, halves, P], F32, name="step%d" % piece)
+            blocks = slice(piece * halves, (piece + 1) * halves) if piece < 2 else slice(piece - 2, PACK, halves)
+            nc.vector.tensor_tensor(
+                step[:], diff[piece // 2][:, blocks, :], keep01[piece // 2][:, blocks, :], ALU.mult
+            )
+            acc = bank(piece, [P, halves, P])
             for i in range(halves):
-                nc.tensor.transpose(acc[:, i * P : (i + 1) * P], step[:, i, :], ident[:])
+                nc.tensor.transpose(acc[:, i, :], step[:, i, :], ident[:])
             back.append(acc)
         out_rows = out_0.rearrange("(p t) v -> p t v", t=PACK)
-        for t in range(PACK):
-            nc.vector.tensor_tensor(res[:, t, :], back[t][:], neg_y2[t], ALU.subtract)
-            if t % 2:
-                nc.sync.dma_start(out=out_rows[:, pairs[t // 2], :], in_=res[:, pairs[t // 2], :])
+        for t in range(2):
+            nc.vector.tensor_tensor(res[:, t, :], both(back[t]), neg_y2[0][:, t, :], ALU.subtract)
+        nc.sync.dma_start(out=out_rows[:, pairs[0], :], in_=res[:, pairs[0], :])
+        for i, vs in enumerate(centres):
+            nc.vector.tensor_tensor(res[:, pairs[1], vs], back[2 + i][:], neg_y2[1][:, :, vs], ALU.subtract)
+        nc.sync.dma_start(out=out_rows[:, pairs[1], :], in_=res[:, pairs[1], :])
 
         o_codes = keep.tile([P, V], U32, name="o_codes", align_bytes=64)
         o_scales = keep.tile([P, V], U8, name="o_scales", align_bytes=64)
-        centres = [slice(0, V // 2), slice(V // 2, V)]
-        res_bf = [keep.tile([P, V // 2, PACK], BF16, name="res_bf%d" % i, align_bytes=64) for i in range(2)]
-        for copy, i in ((nc.scalar.copy, 1), (nc.vector.tensor_copy, 0)):
+        res_bf = keep.tile([P, V, PACK], BF16, name="res_bf", align_bytes=64)
+        for copy, vs in (
+            (nc.scalar.copy, slice(3 * V // 4, V)),
+            (nc.vector.tensor_copy, centres[0]),
+            (nc.vector.tensor_copy, slice(V // 2, 3 * V // 4)),
+        ):
             copy(
-                res_bf[i][:].rearrange("p (c n) t -> p c t n", n=PACK),
-                res[:, :, centres[i]].rearrange("p t (c n) -> p c t n", n=PACK),
+                res_bf[:, vs, :].rearrange("p (c n) t -> p c t n", n=PACK),
+                res[:, :, vs].rearrange("p t (c n) -> p c t n", n=PACK),
             )
-        for i, vs in enumerate(centres):
+        for vs in centres:
             nc.vector.quantize_mx(
                 out=o_codes[:, vs].bitcast(FP8X4),
                 scales=o_scales[:, vs],
-                in_=res_bf[i][:].rearrange("p v t -> p (v t)"),
+                in_=res_bf[:, vs, :].rearrange("p v t -> p (v t)"),
             )
         nc.sync.dma_start(out=out_1[0].rearrange("p n t -> p (n t)").bitcast(I32), in_=o_codes[:].bitcast(I32))
         for q in range(QUADS):

@@ -99,8 +99,6 @@ def tile_picked_zrandla_relu_po_kernel(
 
         ident = keep.tile([P, P], F32, name="ident")
         make_identity(nc, ident[:])
-        preload = keep.tile([P, 1], F32, name="preload")
-        nc.scalar.activation(preload[:], ident[:, 0:1], ACT.Sigmoid)
 
         xs = keep.tile([P, S], U8, name="xs", align_bytes=64)
         nc.vector.tensor_copy(xs[:], xs_table[:].indirect(offs_sb[:]))

@@ -1,3 +1,4 @@
+import math
 from contextlib import ExitStack
 
 import concourse.mybir as mybir
@@ -26,8 +27,9 @@ SCALE_ROWS = 4
 LIST_ROWS = 16
 CHUNK = 128
 CHUNKS = S // CHUNK
-HUGE = 2.0**127
-CLAMP = 24.0
+SHIFT_BITS = 64
+SHIFT = SHIFT_BITS * math.log(2.0)
+CLAMP = SHIFT / 2
 W1_SCALAR_COLS = 192
 
 
@@ -95,10 +97,17 @@ def tile_picked_zrandla_relu_po_kernel(
             xw_table.append(table)
         w2_raw = [load_weight(w2[:, u * N // 2 : (u + 1) * N // 2], "w2_raw%d" % u) for u in range(2)]
         pos_sb = [load_list(src, "pos%d_sb" % d) for d, src in enumerate((pos1, pos2, pos3))]
-        w3_raw = load_weight(w3, "w3_raw")
+        w3_room = keep.tile([P, PACK + 1, N], F32, name="w3_room", align_bytes=64)
+        w3_raw = w3_room[:, 0:PACK, :]
+        nc.sync.dma_start(out=w3_raw, in_=w3.rearrange("(p j) c -> p j c", j=PACK))
 
         ident = keep.tile([P, P], F32, name="ident")
         make_identity(nc, ident[:])
+
+        zero = keep.tile([P, V], F32, name="zero")
+        nc.gpsimd.memset(zero[:], 0.0)
+        e0 = keep.tile([P, V], F32, name="e0")
+        nc.scalar.activation(e0[:], zero[:], ACT.Sigmoid, bias=-SHIFT)
 
         xs = keep.tile([P, S], U8, name="xs", align_bytes=64)
         nc.vector.tensor_copy(xs[:], xs_table[:].indirect(offs_sb[:]))
@@ -168,6 +177,9 @@ def tile_picked_zrandla_relu_po_kernel(
                 in_=h_bf[:, cols, :].rearrange("p n t -> p (n t)"),
             )
         quantise_w2(2, PACK)
+        w3_dealt = dealt_tile("w3_dealt", "w3_dealt")
+        for u in range(2):
+            deal(nc.vector.tensor_copy, w3_dealt, w3_raw[:, :, u * N // 2 : (u + 1) * N // 2], u * N // 2)
 
 
         def second_layer_pass(acc, w_q, t, cols):
@@ -192,6 +204,27 @@ def tile_picked_zrandla_relu_po_kernel(
         def wide(name):
             return keep.tile([P, PACK, V], F32, name=name)
 
+        def pair_tile(name, tag=None):
+            return keep.tile([P, 2, V], F32, name=name, tag=tag or name, align_bytes=64)
+
+        def both(tile):
+            return tile[:, :, :].rearrange("p t v -> p (t v)")
+
+        def picked(rows, d):
+            return rows[:].indirect(pos_sb[d][:])
+
+        s1 = [w3_room[:, PACK - 1 : PACK + 1, 0:V], pair_tile("s1_1")]
+        lead = [w3_room[:, 0:2, n * V : (n + 1) * V] for n in range(2)]
+        cut = [pair_tile("cut%d" % n) for n in range(2)]
+        ref = [pair_tile("ref%d" % n) for n in range(2)]
+        shared = keep.tile([P, PACK, V], F32, name="shared", align_bytes=64)
+        gap = [pair_tile("gap0"), shared[:, 1:3, :]]
+        e1 = [pair_tile("e1_%d" % n) for n in range(2)]
+        e2 = [pair_tile("e2_%d" % n) for n in range(2)]
+
+        def gather_s1(t):
+            nc.scalar.activation(s1[t // 2][:, t % 2, :], picked(score[t], 1), ACT.Copy)
+
         most, last = slice(0, S - CHUNK), slice(S - CHUNK, S)
         acc_most, acc_last, acc_1 = bank(4, [P, S - CHUNK]), bank(5, [P, CHUNK]), bank(6, [P, S])
         for cols in (slice(0, 2 * CHUNK), slice(2 * CHUNK, 3 * CHUNK)):
@@ -199,152 +232,128 @@ def tile_picked_zrandla_relu_po_kernel(
         second_layer_pass(acc_last[:], w2_q, 0, last)
         second_layer_pass(acc_1[:], w2_q, 1, slice(0, S))
         score = [keep.tile([P, S], F32, name="score%d" % t) for t in range(2)]
-        nc.scalar.mul(score[0][:, most], acc_most[:], -1.0)
-        nc.scalar.mul(score[0][:, last], acc_last[:], -1.0)
-        nc.scalar.mul(score[1][:], acc_1[:], -1.0)
-        score.append(second_layer(w2_q, 2, "score2", 7, -1.0))
-        score.append(second_layer(w2_q, 3, "score3", 6, -1.0))
-        w3_dealt = dealt_tile("w3_dealt", "reused")
-        deal(nc.scalar.copy, w3_dealt, w3_raw[:], 0)
-
-        pairs = (slice(0, 2), slice(2, PACK))
-
-        def pair_tile(name, tag=None):
-            return keep.tile([P, 2, V], F32, name=name, tag=tag or name, align_bytes=64)
-
-        def both(tile):
-            return tile[:, :, :].rearrange("p t v -> p (t v)")
-
-        minus = keep.tile([P, V], F32, name="minus")
-        nc.gpsimd.memset(minus[:], -1.0)
-
-        def gather(dst, rows, d, other, op):
-            nc.vector.tensor_tensor(dst, rows[:].indirect(pos_sb[d][:]), other, op)
-
-        def gather_neg_s1(n):
-            for t in range(2):
-                nc.vector.tensor_copy(neg_s1[n][:, t, :], score[2 * n + t][:].indirect(pos_sb[1][:]))
-
-        def gather_a(n):
-            for t in range(2):
-                gather(a[n][:, t, :], score[2 * n + t], 0, neg_s1[n][:, t, :], ALU.subtract)
-
-        second = keep.tile([P, 2, 2, V], F32, name="second", tag="w2_scales", align_bytes=64)
-        neg_s1 = [pair_tile("neg_s1_0"), second[:, 1, :, :]]
-        cut = [pair_tile("cut0")]
-        a = [second[:, 0, :, :]]
-        gather_neg_s1(0)
-        gather_a(0)
-        nc.gpsimd.tensor_scalar(both(cut[0]), both(a[0]), CLAMP, -HUGE, ALU.min, ALU.max)
-        gather_neg_s1(1)
-        a.append(pair_tile("a1", "log_q"))
-        gather_a(1)
+        nc.scalar.mul(score[0][:, most], acc_most[:], 1.0)
+        nc.scalar.mul(score[0][:, last], acc_last[:], 1.0)
+        nc.scalar.mul(score[1][:], acc_1[:], 1.0)
+        score.append(second_layer(w2_q, 2, "score2", 7, 1.0))
+        gather_s1(1)
+        score.append(second_layer(w2_q, 3, "score3", 6, 1.0))
+        gather_s1(2)
+        gather_s1(3)
+        nc.vector.tensor_copy(s1[0][:, 0, :], picked(score[0], 1))
         w3_codes, w3_scales = quantise(w3_dealt, "w3", 1, "w3_codes")
         w3_q = (w3_codes, [w3_scales[:, t * P : (t + 1) * P] for t in range(PACK)])
-        third = keep.tile([P, 3, 2, V], F32, name="third", tag="w3_raw", align_bytes=64)
-        cut.append(third[:, 0, :, :])
-        s2 = [third[:, 1 + n, :, :] for n in range(2)]
-        nc.vector.tensor_scalar_min(both(cut[1]), both(a[1]), CLAMP)
-        for t in range(PACK):
-            gather(s2[t // 2][:, t % 2, :], score[t], 2, minus[:], ALU.mult)
-        q0 = [pair_tile("q0_%d" % n) for n in range(2)]
-        q1 = [pair_tile("q1_%d" % n) for n in range(2)]
 
-        def first_weight(n):
-            nc.scalar.activation(both(q0[n]), both(cut[n]), ACT.Sigmoid, scale=-1.0)
 
-        def second_weight(dst, src):
-            nc.scalar.activation(dst, src, ACT.Sigmoid)
+        def gather_lead(t):
+            nc.vector.tensor_tensor(lead[t // 2][:, t % 2, :], picked(score[t], 0), s1[t // 2][:, t % 2, :], ALU.subtract)
 
-        def features(t):
-            feat.append(second_layer(w3_q, t, "feat%d" % t, 1 + t, 1.0))
+        def gather_gap(t):
+            nc.vector.tensor_tensor(gap[t // 2][:, t % 2, :], picked(score[t], 2), ref[t // 2][:, t % 2, :], ALU.subtract)
+
+        def make_cut(n):
+            nc.vector.tensor_scalar_max(cut[n][:], lead[n], -CLAMP)
+
+        def make_ref(n):
+            nc.vector.scalar_tensor_tensor(ref[n][:], lead[n], -CLAMP, s1[n][:, :, :], ALU.max, ALU.add)
+
+        gather_lead(0)
+        gather_lead(1)
+        gather_lead(2)
+        make_ref(0)
+        gather_lead(3)
+        make_cut(0)
+        gather_gap(0)
+        make_ref(1)
+        gather_gap(1)
+        make_cut(1)
+        gather_gap(2)
+        gather_gap(3)
 
         feat = []
-        first_weight(0)
-        second_weight(both(q1[0]), both(cut[0]))
+
+        def features(t):
+            feat.append(second_layer(w3_q, t, "feat%d" % t, 1 + t, 2.0 ** (SHIFT_BITS // 2)))
+
+        z = [[pair_tile("z0_0")], [pair_tile("z1_%d" % d) for d in range(3)]]
+
+        def gather_first(t):
+            nc.scalar.activation(z[t // 2][0][:, t % 2, :], picked(feat[t], 0), ACT.Copy, scale=e0[:, 0:1])
+
         features(0)
-        features(1)
-        first_weight(1)
-        features(2)
-        second_weight(q1[1][:, 0, :], cut[1][:, 0, :])
-        features(PACK - 1)
-        def add_turned(acc, terms, opens, closes):
+        for t in range(1, PACK):
+            features(t)
+            if t == PACK - 1:
+                nc.scalar.activation(both(e1[0]), both(cut[0]), ACT.Sigmoid, scale=-1.0, bias=-SHIFT)
+            gather_first(t - 1)
+        nc.scalar.activation(both(e2[0]), both(gap[0]), ACT.Sigmoid, bias=-SHIFT)
+        nc.scalar.activation(both(e1[1]), both(cut[1]), ACT.Sigmoid, scale=-1.0, bias=-SHIFT)
+        nc.scalar.activation(both(e2[1]), both(gap[1]), ACT.Sigmoid, bias=-SHIFT)
+
+        halves = V // P
+
+        def add_turned(acc, terms):
             for n, (t, rows) in enumerate(terms):
                 for i in range(halves):
                     nc.tensor.matmul(
                         acc[:, (t % 2) * halves + i, :],
                         rows[:, i * P : (i + 1) * P],
                         ident[:],
-                        start=(opens and n == 0 and i == 0),
-                        stop=(closes and n == len(terms) - 1 and i == halves - 1),
+                        start=(n == 0 and i == 0),
+                        stop=(n == len(terms) - 1 and i == halves - 1),
                         is_transpose=True,
                     )
 
         def by_t(tile):
             return [(t, tile[:, t, :]) for t in range(2)]
 
-        halves = V // P
-        c_turned = [bank(6 + n, [P, 2 * halves, P]) for n in range(2)]
+        den = [bank(6 + n, [P, 2 * halves, P]) for n in range(2)]
         for n in range(2):
-            add_turned(c_turned[n], by_t(neg_s1[n]) + by_t(cut[n]) + by_t(s2[n]), True, False)
-        log_both = keep.tile([P, 2, 2, V], F32, name="log_q", tag="log_q", align_bytes=64)
-        log_q = [log_both[:, n, :, :] for n in range(2)]
+            add_turned(den[n], by_t(e1[n]) + by_t(e2[n]))
+        root = [both(shared[:, 0:2, :]), both(pair_tile("root1"))]
+        inv = [keep.tile([P, 2 * halves, P], F32, name="inv%d" % n) for n in range(2)]
         for n in range(2):
-            nc.scalar.activation(both(log_q[n]), both(q0[n]), ACT.Ln)
-        second_weight(q1[1][:, 1, :], cut[1][:, 1, :])
+            nc.scalar.activation(root[n], both(den[n]), ACT.Abs_reciprocal_sqrt, scale=2.0**SHIFT_BITS, bias=1.0)
+        for n in range(2):
+            nc.scalar.activation(both(inv[n]), root[n], ACT.Square, scale=2.0 ** (SHIFT_BITS // 4))
 
-        keep01 = []
+        z[0].extend([pair_tile("z0_1", "gap0"), shared[:, 2:PACK, :]])
+        num = []
         for n in range(2):
-            add_turned(c_turned[n], by_t(log_q[n]), False, True)
-            weight = keep.tile([P, 2 * halves, P], F32, name="keep01_%d" % n)
-            nc.scalar.activation(weight[:], c_turned[n][:], ACT.Sigmoid, scale=-1.0)
-            keep01.append(weight)
+            if n == 0:
+                nc.vector.tensor_tensor(z[1][0][:, 1, :], picked(feat[3], 0), e0[:], ALU.mult)
+            for d, e in ((1, e1[n]), (2, e2[n])):
+                for t in range(2):
+                    nc.vector.tensor_tensor(z[n][d][:, t, :], picked(feat[2 * n + t], d), e[:, t, :], ALU.mult)
+            acc = bank(5 + n, [P, 2 * halves, P])
+            add_turned(acc, by_t(z[n][0]) + by_t(z[n][1]) + by_t(z[n][2]))
+            num.append(acc)
 
         res = wide("res")
-        diff, neg_y2 = [], []
-        for n, ts in enumerate(pairs):
-            last = pair_tile("neg_y2_%d" % n)
-            z = keep.tile([P, 2, 2, V], F32, name="z%d" % n, tag=("z0", "q0_0")[n], align_bytes=64)
-            for t in range(ts.start, ts.stop):
-                gather(last[:, t % 2, :], feat[t], 2, minus[:], ALU.mult)
-            for d, q in enumerate((q0[n], q1[n])):
-                for t in range(ts.start, ts.stop):
-                    gather(z[:, d, t % 2, :], feat[t], d, q[:, t % 2, :], ALU.mult)
-            neg_y2.append(last)
-            first, second = by_t(z[:, 0, :, :]), by_t(z[:, 1, :, :])
-            acc = bank((5, 4)[n], [P, 2 * halves, P])
-            add_turned(acc, first[0:1] + by_t(last) + first[1:2] + second, True, True)
-            diff.append(acc)
-
-        centres = [slice(0, V // 2), slice(V // 2, V)]
-        back = []
-        for piece in range(PACK):
-            step = keep.tile([P, halves, P], F32, name="step%d" % piece)
-            blocks = slice(piece * halves, (piece + 1) * halves) if piece < 2 else slice(piece - 2, PACK, halves)
-            nc.vector.tensor_tensor(
-                step[:], diff[piece // 2][:, blocks, :], keep01[piece // 2][:, blocks, :], ALU.mult
-            )
-            acc = bank(piece, [P, halves, P])
-            for i in range(halves):
-                nc.tensor.transpose(acc[:, i, :], step[:, i, :], ident[:])
-            back.append(acc)
         out_rows = out_0.rearrange("(p t) v -> p t v", t=PACK)
-        for t in range(2):
-            nc.vector.tensor_tensor(res[:, t, :], both(back[t]), neg_y2[0][:, t, :], ALU.subtract)
-        nc.sync.dma_start(out=out_rows[:, pairs[0], :], in_=res[:, pairs[0], :])
+        centres = [slice(0, V // 2), slice(V // 2, V)]
+        mean = keep.tile([P, 2 * halves, P], F32, name="mean0")
+        nc.vector.tensor_tensor(mean[:], num[0][:], inv[0][:], ALU.mult)
+        back = bank(1, [P, 2 * halves, P])
+        for j in range(2 * halves):
+            nc.tensor.transpose(back[:, j, :], mean[:, j, :], ident[:])
+        nc.scalar.copy(both(res[:, 0:2, :]), back[:].rearrange("p j v -> p (j v)"))
+        nc.sync.dma_start(out=out_rows[:, 0:2, :], in_=res[:, 0:2, :])
         for i, vs in enumerate(centres):
-            nc.vector.tensor_tensor(res[:, pairs[1], vs], back[2 + i][:], neg_y2[1][:, :, vs], ALU.subtract)
-        nc.sync.dma_start(out=out_rows[:, pairs[1], :], in_=res[:, pairs[1], :])
+            blocks = slice(i, 2 * halves, halves)
+            mean = keep.tile([P, 2, P], F32, name="mean1_%d" % i)
+            nc.vector.tensor_tensor(mean[:], num[1][:, blocks, :], inv[1][:, blocks, :], ALU.mult)
+            back = bank(2 + i, [P, 2, P])
+            for t in range(2):
+                nc.tensor.transpose(back[:, t, :], mean[:, t, :], ident[:])
+            nc.scalar.copy(res[:, 2:PACK, vs], back[:])
+        nc.sync.dma_start(out=out_rows[:, 2:PACK, :], in_=res[:, 2:PACK, :])
 
         o_codes = keep.tile([P, V], U32, name="o_codes", align_bytes=64)
         o_scales = keep.tile([P, V], U8, name="o_scales", align_bytes=64)
         res_bf = keep.tile([P, V, PACK], BF16, name="res_bf", align_bytes=64)
-        for copy, vs in (
-            (nc.scalar.copy, slice(3 * V // 4, V)),
-            (nc.vector.tensor_copy, centres[0]),
-            (nc.vector.tensor_copy, slice(V // 2, 3 * V // 4)),
-        ):
-            copy(
+        for vs in centres:
+            nc.vector.tensor_copy(
                 res_bf[:, vs, :].rearrange("p (c n) t -> p c t n", n=PACK),
                 res[:, :, vs].rearrange("p t (c n) -> p c t n", n=PACK),
             )

@@ -27,7 +27,7 @@ SCALE_ROWS = 4
 LIST_ROWS = 16
 CHUNK = 128
 CHUNKS = S // CHUNK
-SHIFT_BITS = 64
+SHIFT_BITS = 48
 SHIFT = SHIFT_BITS * math.log(2.0)
 CLAMP = SHIFT / 2
 W1_SCALAR_COLS = 192
@@ -96,17 +96,17 @@ def tile_picked_zrandla_relu_po_kernel(
             )
             xw_table.append(table)
         w2_raw = [load_weight(w2[:, u * N // 2 : (u + 1) * N // 2], "w2_raw%d" % u) for u in range(2)]
-        pos_sb = [load_list(src, "pos%d_sb" % d) for d, src in enumerate((pos1, pos2, pos3))]
         w3_room = keep.tile([P, PACK + 1, N], F32, name="w3_room", align_bytes=64)
         w3_raw = w3_room[:, 0:PACK, :]
         nc.sync.dma_start(out=w3_raw, in_=w3.rearrange("(p j) c -> p j c", j=PACK))
+        pos_sb = [load_list(src, "pos%d_sb" % d) for d, src in enumerate((pos1, pos2, pos3))]
 
         ident = keep.tile([P, P], F32, name="ident")
         make_identity(nc, ident[:])
 
-        zero = keep.tile([P, V], F32, name="zero")
+        zero = keep.tile([P, V // 2], F32, name="zero")
         nc.gpsimd.memset(zero[:], 0.0)
-        e0 = keep.tile([P, V], F32, name="e0")
+        e0 = keep.tile([P, V // 2], F32, name="e0")
         nc.scalar.activation(e0[:], zero[:], ACT.Sigmoid, bias=-SHIFT)
 
         xs = keep.tile([P, S], U8, name="xs", align_bytes=64)
@@ -120,8 +120,8 @@ def tile_picked_zrandla_relu_po_kernel(
             deal(nc.scalar.copy, w1_dealt, w1_raw[g][:, :, 0:W1_SCALAR_COLS], 0)
             deal(nc.vector.tensor_copy, w1_dealt, w1_raw[g][:, :, W1_SCALAR_COLS:H], W1_SCALAR_COLS)
             w1_q.append(quantise(w1_dealt, "w1_%d" % g, 1, "w1_codes%d" % g))
-        for u in range(2):
-            entries = slice(u * S // 2, (u + 1) * S // 2)
+        for u in range(CHUNKS):
+            entries = slice(u * CHUNK, (u + 1) * CHUNK)
             nc.vector.tensor_copy(
                 xw[1][:, entries],
                 xw_table[1][:].indirect(offs_sb[:, entries.start // LIST_ROWS : entries.stop // LIST_ROWS]),
@@ -287,6 +287,12 @@ def tile_picked_zrandla_relu_po_kernel(
                 nc.scalar.activation(both(e1[0]), both(cut[0]), ACT.Sigmoid, scale=-1.0, bias=-SHIFT)
             gather_first(t - 1)
         nc.scalar.activation(both(e2[0]), both(gap[0]), ACT.Sigmoid, bias=-SHIFT)
+        nc.scalar.activation(
+            z[1][0][:, 1, 0 : V // 2],
+            feat[3][:].indirect(pos_sb[0][:, 0 : V // 2 // LIST_ROWS]),
+            ACT.Copy,
+            scale=e0[:, 0:1],
+        )
         nc.scalar.activation(both(e1[1]), both(cut[1]), ACT.Sigmoid, scale=-1.0, bias=-SHIFT)
         nc.scalar.activation(both(e2[1]), both(gap[1]), ACT.Sigmoid, bias=-SHIFT)
 
@@ -321,39 +327,43 @@ def tile_picked_zrandla_relu_po_kernel(
         num = []
         for n in range(2):
             if n == 0:
-                nc.vector.tensor_tensor(z[1][0][:, 1, :], picked(feat[3], 0), e0[:], ALU.mult)
+                nc.vector.tensor_tensor(
+                    z[1][0][:, 1, V // 2 : V],
+                    feat[3][:].indirect(pos_sb[0][:, V // 2 // LIST_ROWS : V // LIST_ROWS]),
+                    e0[:, 0 : V // 2],
+                    ALU.mult,
+                )
             for d, e in ((1, e1[n]), (2, e2[n])):
                 for t in range(2):
                     nc.vector.tensor_tensor(z[n][d][:, t, :], picked(feat[2 * n + t], d), e[:, t, :], ALU.mult)
-            acc = bank(5 + n, [P, 2 * halves, P])
+            acc = bank((5, 0)[n], [P, 2 * halves, P])
             add_turned(acc, by_t(z[n][0]) + by_t(z[n][1]) + by_t(z[n][2]))
             num.append(acc)
 
         res = wide("res")
         out_rows = out_0.rearrange("(p t) v -> p t v", t=PACK)
         centres = [slice(0, V // 2), slice(V // 2, V)]
-        mean = keep.tile([P, 2 * halves, P], F32, name="mean0")
-        nc.vector.tensor_tensor(mean[:], num[0][:], inv[0][:], ALU.mult)
-        back = bank(1, [P, 2 * halves, P])
-        for j in range(2 * halves):
-            nc.tensor.transpose(back[:, j, :], mean[:, j, :], ident[:])
-        nc.scalar.copy(both(res[:, 0:2, :]), back[:].rearrange("p j v -> p (j v)"))
-        nc.sync.dma_start(out=out_rows[:, 0:2, :], in_=res[:, 0:2, :])
-        for i, vs in enumerate(centres):
-            blocks = slice(i, 2 * halves, halves)
-            mean = keep.tile([P, 2, P], F32, name="mean1_%d" % i)
-            nc.vector.tensor_tensor(mean[:], num[1][:, blocks, :], inv[1][:, blocks, :], ALU.mult)
-            back = bank(2 + i, [P, 2, P])
-            for t in range(2):
-                nc.tensor.transpose(back[:, t, :], mean[:, t, :], ident[:])
-            nc.scalar.copy(res[:, 2:PACK, vs], back[:])
-        nc.sync.dma_start(out=out_rows[:, 2:PACK, :], in_=res[:, 2:PACK, :])
+        for n in range(2):
+            rows = slice(2 * n, 2 * n + 2)
+            for i, vs in enumerate(centres):
+                blocks = slice(i, 2 * halves, halves)
+                mean = keep.tile([P, 2, P], F32, name="mean%d_%d" % (n, i))
+                nc.vector.tensor_tensor(mean[:], num[n][:, blocks, :], inv[n][:, blocks, :], ALU.mult)
+                back = bank(1 + 2 * n + i, [P, 2, P])
+                for t in range(2):
+                    nc.tensor.transpose(back[:, t, :], mean[:, t, :], ident[:])
+                nc.scalar.copy(res[:, rows, vs], back[:])
+            nc.sync.dma_start(out=out_rows[:, rows, :], in_=res[:, rows, :])
 
         o_codes = keep.tile([P, V], U32, name="o_codes", align_bytes=64)
         o_scales = keep.tile([P, V], U8, name="o_scales", align_bytes=64)
         res_bf = keep.tile([P, V, PACK], BF16, name="res_bf", align_bytes=64)
-        for vs in centres:
-            nc.vector.tensor_copy(
+        for copy, vs in (
+            (nc.vector.tensor_copy, centres[0]),
+            (nc.scalar.copy, slice(3 * V // 4, V)),
+            (nc.vector.tensor_copy, slice(V // 2, 3 * V // 4)),
+        ):
+            copy(
                 res_bf[:, vs, :].rearrange("p (c n) t -> p c t n", n=PACK),
                 res[:, :, vs].rearrange("p t (c n) -> p c t n", n=PACK),
             )

@@ -278,7 +278,7 @@ def tile_picked_zrandla_relu_po_kernel(
         z = [[pair_tile("z0_0")], [pair_tile("z1_%d" % d) for d in range(3)]]
 
         def gather_first(t):
-            nc.scalar.activation(z[t // 2][0][:, t % 2, :], picked(feat[t], 0), ACT.Copy, scale=e0[:, 0:1])
+            nc.scalar.activation(z[t // 2][0][:, t % 2, :], picked(feat[t], 0), ACT.Copy, scale=2.0**-SHIFT_BITS)
 
         features(0)
         for t in range(1, PACK):
@@ -291,7 +291,7 @@ def tile_picked_zrandla_relu_po_kernel(
             z[1][0][:, 1, 0 : V // 2],
             feat[3][:].indirect(pos_sb[0][:, 0 : V // 2 // LIST_ROWS]),
             ACT.Copy,
-            scale=e0[:, 0:1],
+            scale=2.0**-SHIFT_BITS,
         )
         nc.scalar.activation(both(e1[1]), both(cut[1]), ACT.Sigmoid, scale=-1.0, bias=-SHIFT)
         nc.scalar.activation(both(e2[1]), both(gap[1]), ACT.Sigmoid, bias=-SHIFT)

@@ -78,17 +78,25 @@ def tile_picked_zrandla_relu_po_kernel(
             return codes, scales
 
         xs_table = keep.tile([P, T], U8, name="xs_table")
-        nc.vector.memset(xs_table[:].bitcast(I32), 0)
+        nc.gpsimd.memset(xs_table[:].bitcast(I32), 0)
+
+        def load_scale_rows(r):
+            for g in range(PASSES):
+                first = SCALE_ROWS * g + r
+                nc.sync.dma_start(
+                    out=xs_table[first:P:QUAD, :].bitcast(I32),
+                    in_=x_scales.bitcast(I32)[g, r : QUADS * SCALE_ROWS : SCALE_ROWS, :],
+                )
+
         w1_raw = [load_weight(w1[0:K_PASS, :], "w1_raw0")]
-        for q in range(QUADS):
-            nc.sync.dma_start(
-                out=xs_table[QUAD * q : QUAD * q + SCALE_ROWS * PASSES, :].bitcast(I32),
-                in_=x_scales.bitcast(I32)[:, SCALE_ROWS * q : SCALE_ROWS * (q + 1), :],
-            )
         offs_sb = load_list(offs, "offs_sb")
+        load_scale_rows(0)
+        load_scale_rows(1)
         xw_table = []
         for g in range(PASSES):
             if g == 1:
+                load_scale_rows(2)
+                load_scale_rows(3)
                 w1_raw.append(load_weight(w1[K_PASS:K, :], "w1_raw1"))
             table = keep.tile([P, T], U32, name="xw_table%d" % g)
             nc.sync.dma_start(
@@ -110,12 +118,12 @@ def tile_picked_zrandla_relu_po_kernel(
         nc.scalar.activation(e0[:], zero[:], ACT.Sigmoid, bias=-SHIFT)
 
         xs = keep.tile([P, S], U8, name="xs", align_bytes=64)
-        nc.vector.tensor_copy(xs[:], xs_table[:].indirect(offs_sb[:]))
         w1_q = []
         xw = [keep.tile([P, S], U32, name="xw%d" % g, align_bytes=64) for g in range(PASSES)]
         for g in range(PASSES):
             if g == 1:
                 nc.vector.tensor_copy(xw[0][:], xw_table[0][:].indirect(offs_sb[:]))
+                nc.vector.tensor_copy(xs[:], xs_table[:].indirect(offs_sb[:]))
             w1_dealt = dealt_tile("w1_dealt%d" % g, "w1_dealt%d" % g)
             deal(nc.scalar.copy, w1_dealt, w1_raw[g][:, :, 0:W1_SCALAR_COLS], 0)
             deal(nc.vector.tensor_copy, w1_dealt, w1_raw[g][:, :, W1_SCALAR_COLS:H], W1_SCALAR_COLS)

@@ -112,10 +112,10 @@ def tile_picked_zrandla_relu_po_kernel(
         ident = keep.tile([P, P], F32, name="ident")
         make_identity(nc, ident[:])
 
-        zero = keep.tile([P, V // 2], F32, name="zero")
+        zero = keep.tile([P, 1], F32, name="zero")
         nc.gpsimd.memset(zero[:], 0.0)
-        e0 = keep.tile([P, V // 2], F32, name="e0")
-        nc.scalar.activation(e0[:], zero[:], ACT.Sigmoid, bias=-SHIFT)
+        one = keep.tile([P, 1], F32, name="one")
+        nc.scalar.activation(one[:], zero[:], ACT.Sigmoid, bias=SHIFT)
 
         xs = keep.tile([P, S], U8, name="xs", align_bytes=64)
         w1_q = []
@@ -206,7 +206,7 @@ def tile_picked_zrandla_relu_po_kernel(
             acc = bank(index, [P, S])
             second_layer_pass(acc[:], w_q, t, slice(0, S))
             row = keep.tile([P, S], F32, name=name)
-            nc.scalar.mul(row[:], acc[:], sign)
+            nc.scalar.activation(row[:], acc[:], ACT.Copy, scale=sign)
             return row
 
         def wide(name):
@@ -234,22 +234,31 @@ def tile_picked_zrandla_relu_po_kernel(
             nc.scalar.activation(s1[t // 2][:, t % 2, :], picked(score[t], 1), ACT.Copy)
 
         most, last = slice(0, S - CHUNK), slice(S - CHUNK, S)
-        acc_most, acc_last, acc_1 = bank(4, [P, S - CHUNK]), bank(5, [P, CHUNK]), bank(6, [P, S])
-        for cols in (slice(0, 2 * CHUNK), slice(2 * CHUNK, 3 * CHUNK)):
-            second_layer_pass(acc_most[:, cols], w2_q, 0, cols)
-        second_layer_pass(acc_last[:], w2_q, 0, last)
-        second_layer_pass(acc_1[:], w2_q, 1, slice(0, S))
+        acc_most, acc_last = [bank(4 + 2 * t, [P, S - CHUNK]) for t in range(2)], bank(5, [P, 2, CHUNK])
+        for t in range(2):
+            for cols in (slice(0, 2 * CHUNK), slice(2 * CHUNK, 3 * CHUNK)):
+                second_layer_pass(acc_most[t][:, cols], w2_q, t, cols)
+        for t in range(2):
+            second_layer_pass(acc_last[:, t, :], w2_q, t, last)
         score = [keep.tile([P, S], F32, name="score%d" % t) for t in range(2)]
-        nc.scalar.mul(score[0][:, most], acc_most[:], 1.0)
-        nc.scalar.mul(score[0][:, last], acc_last[:], 1.0)
-        nc.scalar.mul(score[1][:], acc_1[:], 1.0)
+        for t in range(2):
+            nc.scalar.copy(score[t][:, most], acc_most[t][:])
+        for t in range(2):
+            nc.scalar.copy(score[t][:, last], acc_last[:, t, :])
         score.append(second_layer(w2_q, 2, "score2", 7, 1.0))
         gather_s1(1)
-        score.append(second_layer(w2_q, 3, "score3", 6, 1.0))
+        score.append(second_layer(w2_q, 3, "score3", 0, 1.0))
         gather_s1(2)
         gather_s1(3)
         nc.vector.tensor_copy(s1[0][:, 0, :], picked(score[0], 1))
-        w3_codes, w3_scales = quantise(w3_dealt, "w3", 1, "w3_codes")
+        w3_codes = keep.tile([P, K_PASS], U32, name="w3_codes", align_bytes=64)
+        w3_scales = keep.tile([P, K_PASS], U8, name="w3_scales", align_bytes=64)
+        for first, stop in ((0, 1), (1, PACK)):
+            nc.vector.quantize_mx(
+                out=w3_codes[:, first * P : stop * P].bitcast(FP8X4),
+                scales=w3_scales[:, first * P : stop * P],
+                in_=w3_dealt[:, first:stop, :, :].rearrange("p t m j -> p (t m j)"),
+            )
         w3_q = (w3_codes, [w3_scales[:, t * P : (t + 1) * P] for t in range(PACK)])
 
 
@@ -283,7 +292,7 @@ def tile_picked_zrandla_relu_po_kernel(
         def features(t):
             feat.append(second_layer(w3_q, t, "feat%d" % t, 1 + t, 2.0 ** (SHIFT_BITS // 2)))
 
-        z = [[pair_tile("z0_0")], [pair_tile("z1_%d" % d) for d in range(3)]]
+        z = [[pair_tile("z0_0")], [pair_tile("z1_0"), shared[:, 2:PACK, :], pair_tile("z1_2")]]
 
         def gather_first(t):
             nc.scalar.activation(z[t // 2][0][:, t % 2, :], picked(feat[t], 0), ACT.Copy, scale=2.0**-SHIFT_BITS)
@@ -295,12 +304,7 @@ def tile_picked_zrandla_relu_po_kernel(
                 nc.scalar.activation(both(e1[0]), both(cut[0]), ACT.Sigmoid, scale=-1.0, bias=-SHIFT)
             gather_first(t - 1)
         nc.scalar.activation(both(e2[0]), both(gap[0]), ACT.Sigmoid, bias=-SHIFT)
-        nc.scalar.activation(
-            z[1][0][:, 1, 0 : V // 2],
-            feat[3][:].indirect(pos_sb[0][:, 0 : V // 2 // LIST_ROWS]),
-            ACT.Copy,
-            scale=2.0**-SHIFT_BITS,
-        )
+        gather_first(PACK - 1)
         nc.scalar.activation(both(e1[1]), both(cut[1]), ACT.Sigmoid, scale=-1.0, bias=-SHIFT)
         nc.scalar.activation(both(e2[1]), both(gap[1]), ACT.Sigmoid, bias=-SHIFT)
 
@@ -324,23 +328,16 @@ def tile_picked_zrandla_relu_po_kernel(
         den = [bank(6 + n, [P, 2 * halves, P]) for n in range(2)]
         for n in range(2):
             add_turned(den[n], by_t(e1[n]) + by_t(e2[n]))
-        root = [both(shared[:, 0:2, :]), both(pair_tile("root1"))]
+        root = [tile.rearrange("p t (i v) -> p (t i) v", v=P) for tile in (shared[:, 0:2, :], pair_tile("root1")[:])]
         inv = [keep.tile([P, 2 * halves, P], F32, name="inv%d" % n) for n in range(2)]
         for n in range(2):
-            nc.scalar.activation(root[n], both(den[n]), ACT.Abs_reciprocal_sqrt, scale=2.0**SHIFT_BITS, bias=1.0)
+            nc.scalar.activation(root[n], den[n][:], ACT.Abs_reciprocal_sqrt, scale=2.0**SHIFT_BITS, bias=one[:])
         for n in range(2):
-            nc.scalar.activation(both(inv[n]), root[n], ACT.Square, scale=2.0 ** (SHIFT_BITS // 4))
+            nc.scalar.activation(inv[n][:], root[n], ACT.Square, scale=2.0 ** (SHIFT_BITS // 4))
 
-        z[0].extend([pair_tile("z0_1", "gap0"), shared[:, 2:PACK, :]])
+        z[0].extend([pair_tile("z0_1", "gap0"), pair_tile("z0_2")])
         num = []
         for n in range(2):
-            if n == 0:
-                nc.vector.tensor_tensor(
-                    z[1][0][:, 1, V // 2 : V],
-                    feat[3][:].indirect(pos_sb[0][:, V // 2 // LIST_ROWS : V // LIST_ROWS]),
-                    e0[:, 0 : V // 2],
-                    ALU.mult,
-                )
             for d, e in ((1, e1[n]), (2, e2[n])):
                 for t in range(2):
                     nc.vector.tensor_tensor(z[n][d][:, t, :], picked(feat[2 * n + t], d), e[:, t, :], ALU.mult)

@@ -333,7 +333,11 @@ def tile_picked_zrandla_relu_po_kernel(
         for n in range(2):
             nc.scalar.activation(root[n], den[n][:], ACT.Abs_reciprocal_sqrt, scale=2.0**SHIFT_BITS, bias=one[:])
         for n in range(2):
-            nc.scalar.activation(inv[n][:], root[n], ACT.Square, scale=2.0 ** (SHIFT_BITS // 4))
+            for i in range(halves):
+                blocks = slice(i, 2 * halves, halves)
+                nc.scalar.activation(
+                    inv[n][:, blocks, :], root[n][:, blocks, :], ACT.Square, scale=2.0 ** (SHIFT_BITS // 4)
+                )
 
         z[0].extend([pair_tile("z0_1", "gap0"), pair_tile("z0_2")])
         num = []

import math
from contextlib import ExitStack

import concourse.mybir as mybir
from concourse.masks import make_identity

K, T, S, V, H, N = 1024, 2048, 512, 256, 512, 512
FLOPS = 2 * S * (K * H + 2 * H * N)

F32 = mybir.dt.float32
BF16 = mybir.dt.bfloat16
I32 = mybir.dt.int32
U32 = mybir.dt.uint32
U16 = mybir.dt.uint16
U8 = mybir.dt.uint8
FP8X4 = mybir.dt.float8_e4m3fn_x4
ACT = mybir.ActivationFunctionType
ALU = mybir.AluOpType

P = 128
PACK = 4
K_PASS = P * PACK
PASSES = K // K_PASS
QUADS = 4
QUAD = P // QUADS
SCALE_ROWS = 4
LIST_ROWS = 16
CHUNK = 128
CHUNKS = S // CHUNK
SHIFT_BITS = 48
SHIFT = SHIFT_BITS * math.log(2.0)
CLAMP = SHIFT / 2
W1_SCALAR_COLS = 192


def tile_picked_zrandla_relu_po_kernel(
    tc, x_words, x_scales, w1, w2, w3, offs, pos1, pos2, pos3, out_0, out_1, out_2
):
    nc = tc.nc
    with ExitStack() as ctx:
        keep = ctx.enter_context(tc.tile_pool(name="keep", bufs=1))
        psum = ctx.enter_context(tc.psum_pool(name="psum", bufs=1))

        def bank(index, shape):
            return psum.tile(shape, F32, name="bank%d" % index)

        def load_list(src, name):
            tile = keep.tile(list(src.shape), U16, name=name)
            nc.sync.dma_start(tile[:], src)
            return tile

        def load_weight(rows, name):
            raw = keep.tile([P, PACK, rows.shape[1]], F32, name=name, tag=name, align_bytes=64)
            nc.sync.dma_start(out=raw[:], in_=rows.rearrange("(p j) c -> p j c", j=PACK))
            return raw

        def dealt_tile(name, tag):
            return keep.tile([P, PACK, P, PACK], BF16, name=name, tag=tag, align_bytes=64)

        def deal(copy, dealt, raw, first_col):
            first, count = first_col // PACK, raw.shape[2] // PACK
            copy(
                dealt[:, :, first : first + count, :].rearrange("p t m j -> p m j t"),
                raw.rearrange("p j (m t) -> p m j t", t=PACK),
            )

        def quantise(dealt, name, pieces, tag):
            codes = keep.tile([P, K_PASS], U32, name=name + "_codes", tag=tag, align_bytes=64)
            scales = keep.tile([P, K_PASS], U8, name=name + "_scales", align_bytes=64)
            width = K_PASS // pieces
            values = dealt[:].rearrange("p t m j -> p (t m j)")
            for i in range(pieces):
                nc.vector.quantize_mx(
                    out=codes[:, i * width : (i + 1) * width].bitcast(FP8X4),
                    scales=scales[:, i * width : (i + 1) * width],
                    in_=values[:, PACK * i * width : PACK * (i + 1) * width],
                )
            return codes, scales

        xs_table = keep.tile([P, T], U8, name="xs_table")
        nc.gpsimd.memset(xs_table[:].bitcast(I32), 0)

        def load_scale_rows(r):
            for g in range(PASSES):
                first = SCALE_ROWS * g + r
                nc.sync.dma_start(
                    out=xs_table[first:P:QUAD, :].bitcast(I32),
                    in_=x_scales.bitcast(I32)[g, r : QUADS * SCALE_ROWS : SCALE_ROWS, :],
                )

        w1_raw = [load_weight(w1[0:K_PASS, :], "w1_raw0")]
        offs_sb = load_list(offs, "offs_sb")
        load_scale_rows(0)
        load_scale_rows(1)
        xw_table = []
        for g in range(PASSES):
            if g == 1:
                load_scale_rows(2)
                load_scale_rows(3)
                w1_raw.append(load_weight(w1[K_PASS:K, :], "w1_raw1"))
            table = keep.tile([P, T], U32, name="xw_table%d" % g)
            nc.sync.dma_start(
                out=table[:].bitcast(I32), in_=x_words[g].rearrange("p n t -> p (n t)").bitcast(I32)
            )
            xw_table.append(table)
        w2_raw = [load_weight(w2[:, u * N // 2 : (u + 1) * N // 2], "w2_raw%d" % u) for u in range(2)]
        w3_room = keep.tile([P, PACK + 1, N], F32, name="w3_room", align_bytes=64)
        w3_raw = w3_room[:, 0:PACK, :]
        nc.sync.dma_start(out=w3_raw, in_=w3.rearrange("(p j) c -> p j c", j=PACK))
        pos_sb = [load_list(src, "pos%d_sb" % d) for d, src in enumerate((pos1, pos2, pos3))]

        ident = keep.tile([P, P], F32, name="ident")
        make_identity(nc, ident[:])

        zero = keep.tile([P, 1], F32, name="zero")
        nc.gpsimd.memset(zero[:], 0.0)
        one = keep.tile([P, 1], F32, name="one")
        nc.scalar.activation(one[:], zero[:], ACT.Sigmoid, bias=SHIFT)

        xs = keep.tile([P, S], U8, name="xs", align_bytes=64)
        w1_q = []
        xw = [keep.tile([P, S], U32, name="xw%d" % g, align_bytes=64) for g in range(PASSES)]
        for g in range(PASSES):
            if g == 1:
                nc.vector.tensor_copy(xw[0][:], xw_table[0][:].indirect(offs_sb[:]))
                nc.vector.tensor_copy(xs[:], xs_table[:].indirect(offs_sb[:]))
            w1_dealt = dealt_tile("w1_dealt%d" % g, "w1_dealt%d" % g)
            deal(nc.scalar.copy, w1_dealt, w1_raw[g][:, :, 0:W1_SCALAR_COLS], 0)
            deal(nc.vector.tensor_copy, w1_dealt, w1_raw[g][:, :, W1_SCALAR_COLS:H], W1_SCALAR_COLS)
            w1_q.append(quantise(w1_dealt, "w1_%d" % g, 1, "w1_codes%d" % g))
        for u in range(CHUNKS):
            entries = slice(u * CHUNK, (u + 1) * CHUNK)
            nc.vector.tensor_copy(
                xw[1][:, entries],
                xw_table[1][:].indirect(offs_sb[:, entries.start // LIST_ROWS : entries.stop // LIST_ROWS]),
            )

        h_bf = keep.tile([P, S, PACK], BF16, name="h_bf", align_bytes=64)
        h_scales = keep.tile([P, S], U8, name="h_scales", align_bytes=64)
        h_banks = [bank(c, [P, PACK, CHUNK]) for c in range(CHUNKS)]

        def first_layer_pass(c, t, g):
            cols = slice(c * CHUNK, (c + 1) * CHUNK)
            chans = slice(t * P, (t + 1) * P)
            codes, scales = w1_q[g]
            nc.tensor.matmul_mx(
                out=h_banks[c][:, t, :],
                lhsT=codes[:, chans].bitcast(FP8X4),
                lhsT_scale=scales[:, chans],
                rhs=xw[g][:, cols].bitcast(FP8X4),
                rhs_scale=xs[SCALE_ROWS * g : P, cols],
                start=(g == 0 and t == 0),
                stop=(g == PASSES - 1 and t == PACK - 1),
            )

        for g in range(PASSES):
            for c in range(CHUNKS):
                for t in range(PACK):
                    first_layer_pass(c, t, g)

        w2_dealt = dealt_tile("w2_dealt", "w2_dealt")
        w2_codes = keep.tile([P, K_PASS], U32, name="w2_codes", tag="reused", align_bytes=64)
        w2_scales = keep.tile([P, K_PASS], U8, name="w2_scales", tag="w2_scales", align_bytes=64)
        w2_q = (w2_codes, [w2_scales[:, t * P : (t + 1) * P] for t in range(PACK)])

        def quantise_w2(first, stop):
            nc.vector.quantize_mx(
                out=w2_codes[:, first * P : stop * P].bitcast(FP8X4),
                scales=w2_scales[:, first * P : stop * P],
                in_=w2_dealt[:, first:stop, :, :].rearrange("p t m j -> p (t m j)"),
            )

        for u, raw in enumerate(w2_raw):
            deal(nc.vector.tensor_copy, w2_dealt, raw[:], u * N // 2)
        h_codes = keep.tile([P, S], U32, name="h_codes", tag="w2_raw1", align_bytes=64)
        quantise_w2(0, 1)
        for c in range(CHUNKS):
            cols = slice(c * CHUNK, (c + 1) * CHUNK)
            if c == CHUNKS - 1:
                quantise_w2(1, 2)
            nc.scalar.activation(h_bf[:, cols, :], h_banks[c][:].rearrange("p t n -> p n t"), ACT.Relu)
            nc.vector.quantize_mx(
                out=h_codes[:, cols].bitcast(FP8X4),
                scales=h_scales[:, cols],
                in_=h_bf[:, cols, :].rearrange("p n t -> p (n t)"),
            )
        quantise_w2(2, PACK)
        w3_dealt = dealt_tile("w3_dealt", "w3_dealt")
        for u in range(2):
            deal(nc.vector.tensor_copy, w3_dealt, w3_raw[:, :, u * N // 2 : (u + 1) * N // 2], u * N // 2)


        def second_layer_pass(acc, w_q, t, cols):
            codes, planes = w_q
            nc.tensor.matmul_mx(
                out=acc,
                lhsT=codes[:, t * P : (t + 1) * P].bitcast(FP8X4),
                lhsT_scale=planes[t],
                rhs=h_codes[:, cols].bitcast(FP8X4),
                rhs_scale=h_scales[:, cols],
                start=True,
                stop=True,
            )

        def second_layer(w_q, t, name, index, sign):
            acc = bank(index, [P, S])
            second_layer_pass(acc[:], w_q, t, slice(0, S))
            row = keep.tile([P, S], F32, name=name)
            nc.scalar.activation(row[:], acc[:], ACT.Copy, scale=sign)
            return row

        def wide(name):
            return keep.tile([P, PACK, V], F32, name=name)

        def pair_tile(name, tag=None):
            return keep.tile([P, 2, V], F32, name=name, tag=tag or name, align_bytes=64)

        def both(tile):
            return tile[:, :, :].rearrange("p t v -> p (t v)")

        def picked(rows, d):
            return rows[:].indirect(pos_sb[d][:])

        s1 = [w3_room[:, PACK - 1 : PACK + 1, 0:V], pair_tile("s1_1")]
        lead = [w3_room[:, 0:2, n * V : (n + 1) * V] for n in range(2)]
        cut = [pair_tile("cut%d" % n) for n in range(2)]
        ref = [pair_tile("ref%d" % n) for n in range(2)]
        shared = keep.tile([P, PACK, V], F32, name="shared", align_bytes=64)
        gap = [pair_tile("gap0"), shared[:, 1:3, :]]
        e1 = [pair_tile("e1_%d" % n) for n in range(2)]
        e2 = [pair_tile("e2_%d" % n) for n in range(2)]

        def gather_s1(t):
            nc.scalar.activation(s1[t // 2][:, t % 2, :], picked(score[t], 1), ACT.Copy)

        most, last = slice(0, S - CHUNK), slice(S - CHUNK, S)
        acc_most, acc_last = [bank(4 + 2 * t, [P, S - CHUNK]) for t in range(2)], bank(5, [P, 2, CHUNK])
        for t in range(2):
            for cols in (slice(0, 2 * CHUNK), slice(2 * CHUNK, 3 * CHUNK)):
                second_layer_pass(acc_most[t][:, cols], w2_q, t, cols)
        for t in range(2):
            second_layer_pass(acc_last[:, t, :], w2_q, t, last)
        score = [keep.tile([P, S], F32, name="score%d" % t) for t in range(2)]
        for t in range(2):
            nc.scalar.copy(score[t][:, most], acc_most[t][:])
        for t in range(2):
            nc.scalar.copy(score[t][:, last], acc_last[:, t, :])
        score.append(second_layer(w2_q, 2, "score2", 7, 1.0))
        gather_s1(1)
        score.append(second_layer(w2_q, 3, "score3", 0, 1.0))
        gather_s1(2)
        gather_s1(3)
        nc.vector.tensor_copy(s1[0][:, 0, :], picked(score[0], 1))
        w3_codes = keep.tile([P, K_PASS], U32, name="w3_codes", align_bytes=64)
        w3_scales = keep.tile([P, K_PASS], U8, name="w3_scales", align_bytes=64)
        for first, stop in ((0, 1), (1, PACK)):
            nc.vector.quantize_mx(
                out=w3_codes[:, first * P : stop * P].bitcast(FP8X4),
                scales=w3_scales[:, first * P : stop * P],
                in_=w3_dealt[:, first:stop, :, :].rearrange("p t m j -> p (t m j)"),
            )
        w3_q = (w3_codes, [w3_scales[:, t * P : (t + 1) * P] for t in range(PACK)])


        def gather_lead(t):
            nc.vector.tensor_tensor(lead[t // 2][:, t % 2, :], picked(score[t], 0), s1[t // 2][:, t % 2, :], ALU.subtract)

        def gather_gap(t):
            nc.vector.tensor_tensor(gap[t // 2][:, t % 2, :], picked(score[t], 2), ref[t // 2][:, t % 2, :], ALU.subtract)

        def make_cut(n):
            nc.vector.tensor_scalar_max(cut[n][:], lead[n], -CLAMP)

        def make_ref(n):
            nc.vector.scalar_tensor_tensor(ref[n][:], lead[n], -CLAMP, s1[n][:, :, :], ALU.max, ALU.add)

        gather_lead(0)
        gather_lead(1)
        gather_lead(2)
        make_ref(0)
        gather_lead(3)
        make_cut(0)
        gather_gap(0)
        make_ref(1)
        gather_gap(1)
        make_cut(1)
        gather_gap(2)
        gather_gap(3)

        feat = []

        def features(t):
            feat.append(second_layer(w3_q, t, "feat%d" % t, 1 + t, 2.0 ** (SHIFT_BITS // 2)))

        z = [[pair_tile("z0_0")], [pair_tile("z1_0"), shared[:, 2:PACK, :], pair_tile("z1_2")]]

        def gather_first(t):
            nc.scalar.activation(z[t // 2][0][:, t % 2, :], picked(feat[t], 0), ACT.Copy, scale=2.0**-SHIFT_BITS)

        features(0)
        for t in range(1, PACK):
            features(t)
            if t == PACK - 1:
                nc.scalar.activation(both(e1[0]), both(cut[0]), ACT.Sigmoid, scale=-1.0, bias=-SHIFT)
            gather_first(t - 1)
        nc.scalar.activation(both(e2[0]), both(gap[0]), ACT.Sigmoid, bias=-SHIFT)
        gather_first(PACK - 1)
        nc.scalar.activation(both(e1[1]), both(cut[1]), ACT.Sigmoid, scale=-1.0, bias=-SHIFT)
        nc.scalar.activation(both(e2[1]), both(gap[1]), ACT.Sigmoid, bias=-SHIFT)

        halves = V // P

        def add_turned(acc, terms):
            for n, (t, rows) in enumerate(terms):
                for i in range(halves):
                    nc.tensor.matmul(
                        acc[:, (t % 2) * halves + i, :],
                        rows[:, i * P : (i + 1) * P],
                        ident[:],
                        start=(n == 0 and i == 0),
                        stop=(n == len(terms) - 1 and i == halves - 1),
                        is_transpose=True,
                    )

        def by_t(tile):
            return [(t, tile[:, t, :]) for t in range(2)]

        den = [bank(6 + n, [P, 2 * halves, P]) for n in range(2)]
        for n in range(2):
            add_turned(den[n], by_t(e1[n]) + by_t(e2[n]))
        root = [tile.rearrange("p t (i v) -> p (t i) v", v=P) for tile in (shared[:, 0:2, :], pair_tile("root1")[:])]
        inv = [keep.tile([P, 2 * halves, P], F32, name="inv%d" % n) for n in range(2)]
        for n in range(2):
            nc.scalar.activation(root[n], den[n][:], ACT.Abs_reciprocal_sqrt, scale=2.0**SHIFT_BITS, bias=one[:])
        for n in range(2):
            for i in range(halves):
                blocks = slice(i, 2 * halves, halves)
                nc.scalar.activation(
                    inv[n][:, blocks, :], root[n][:, blocks, :], ACT.Square, scale=2.0 ** (SHIFT_BITS // 4)
                )

        z[0].extend([pair_tile("z0_1", "gap0"), pair_tile("z0_2")])
        num = []
        for n in range(2):
            for d, e in ((1, e1[n]), (2, e2[n])):
                for t in range(2):
                    nc.vector.tensor_tensor(z[n][d][:, t, :], picked(feat[2 * n + t], d), e[:, t, :], ALU.mult)
            acc = bank((5, 0)[n], [P, 2 * halves, P])
            add_turned(acc, by_t(z[n][0]) + by_t(z[n][1]) + by_t(z[n][2]))
            num.append(acc)

        res = wide("res")
        out_rows = out_0.rearrange("(p t) v -> p t v", t=PACK)
        centres = [slice(0, V // 2), slice(V // 2, V)]
        for n in range(2):
            rows = slice(2 * n, 2 * n + 2)
            for i, vs in enumerate(centres):
                blocks = slice(i, 2 * halves, halves)
                mean = keep.tile([P, 2, P], F32, name="mean%d_%d" % (n, i))
                nc.vector.tensor_tensor(mean[:], num[n][:, blocks, :], inv[n][:, blocks, :], ALU.mult)
                back = bank(1 + 2 * n + i, [P, 2, P])
                for t in range(2):
                    nc.tensor.transpose(back[:, t, :], mean[:, t, :], ident[:])
                nc.scalar.copy(res[:, rows, vs], back[:])
            nc.sync.dma_start(out=out_rows[:, rows, :], in_=res[:, rows, :])

        o_codes = keep.tile([P, V], U32, name="o_codes", align_bytes=64)
        o_scales = keep.tile([P, V], U8, name="o_scales", align_bytes=64)
        res_bf = keep.tile([P, V, PACK], BF16, name="res_bf", align_bytes=64)
        for copy, vs in (
            (nc.vector.tensor_copy, centres[0]),
            (nc.scalar.copy, slice(3 * V // 4, V)),
            (nc.vector.tensor_copy, slice(V // 2, 3 * V // 4)),
        ):
            copy(
                res_bf[:, vs, :].rearrange("p (c n) t -> p c t n", n=PACK),
                res[:, :, vs].rearrange("p t (c n) -> p c t n", n=PACK),
            )
        for vs in centres:
            nc.vector.quantize_mx(
                out=o_codes[:, vs].bitcast(FP8X4),
                scales=o_scales[:, vs],
                in_=res_bf[:, vs, :].rearrange("p v t -> p (v t)"),
            )
        nc.sync.dma_start(out=out_1[0].rearrange("p n t -> p (n t)").bitcast(I32), in_=o_codes[:].bitcast(I32))
        for q in range(QUADS):
            queue = nc.scalar if q % 2 else nc.sync
            queue.dma_start(
                out=out_2[0].bitcast(I32)[SCALE_ROWS * q : SCALE_ROWS * (q + 1), :],
                in_=o_scales[QUAD * q : QUAD * q + SCALE_ROWS, :].bitcast(I32),
            )
